import numpy as np
import ml_dtypes


def mxq(x, axis, fmt="e4m3"):
    dtype, down = {"e4m3": (ml_dtypes.float8_e4m3fn, 7), "e5m2": (ml_dtypes.float8_e5m2, 14)}[fmt]
    v = np.moveaxis(np.asarray(x, np.float32).astype(ml_dtypes.bfloat16).astype(np.float64), axis, -1)
    blocks = v.reshape(v.shape[:-1] + (-1, 32))
    amax = np.abs(blocks).max(-1, keepdims=True)
    byte = np.maximum(np.where(amax > 0, np.frexp(amax)[1] - 1 + 127, 0) - down, 1)
    scale = np.exp2(byte - 127.0)
    codes = (blocks / scale).astype(np.float32).astype(dtype).astype(np.float64)
    return np.moveaxis((codes * scale).reshape(v.shape), -1, axis)


WIDE = False


def mx_kscale(k):
    if not WIDE:
        return np.ones(k)
    levels = np.array([10, -10, 5, -5, 0])
    if k % 512:
        return np.exp2(np.random.permutation(np.resize(levels, k // 32))).repeat(32)
    a = np.empty((k // 512, 16))
    for p in range(k // 512):
        a[p, :8] = np.random.permutation(np.resize(levels, 8))
        for g in range(8):
            far = levels[np.abs(levels - a[p, g]) >= 10]
            a[p, g + 8] = far[np.random.randint(len(far))]
    return np.exp2(a.ravel()).repeat(32)


def f64(x):
    return np.asarray(x).astype(np.float64)


def striped(idx):
    return np.tile(np.asarray(idx).reshape(-1, 16).T, (8, 1)).astype(np.uint16)


def unstriped(offs):
    return offs[:16].T.reshape(-1).astype(np.int64)


E2M1 = np.array([0.0, 0.5, 1.0, 1.5, 2.0, 3.0, 4.0, 6.0, -0.0, -0.5, -1.0, -1.5, -2.0, -3.0, -4.0, -6.0])


def pack_weight(w, fmt):
    k, n = w.shape
    w = f64(np.asarray(w, np.float32).astype(ml_dtypes.bfloat16)).reshape(k // 32, 32, n)
    amax = np.abs(w).max(1)
    if fmt == "e4m3":
        byte = np.frexp(amax)[1] - 1 + 127 - 7
    else:
        mant, ex = np.frexp(amax / 6.0)
        byte = np.where(mant > 0.5, ex, ex - 1) + 127
    byte = np.clip(np.where(amax > 0, byte, 1), 1, 254)
    scaled = (w * np.exp2(127.0 - byte)[:, None, :]).reshape(k, n).astype(np.float32)
    by_word = np.ascontiguousarray(scaled.reshape(k // 512, 128, 4, n).transpose(0, 1, 3, 2))
    if fmt == "e4m3":
        words = by_word.astype(ml_dtypes.float8_e4m3fn).view(np.uint8)
    else:
        c = by_word.astype(ml_dtypes.float4_e2m1fn).view(np.uint8) & 0xF
        words = (c[..., 0::2] | (c[..., 1::2] << 4)).reshape(k // 512, 128, 2 * n)
    return np.ascontiguousarray(words), np.ascontiguousarray(byte.astype(np.uint8).reshape(k // 512, 16, n))


def unpack_weight(words, scales, fmt):
    g, _, n = scales.shape
    words = np.ascontiguousarray(words).reshape(g, 128, n, -1)
    if fmt == "e4m3":
        vals = words.view(ml_dtypes.float8_e4m3fn).astype(np.float64)
    else:
        nib = np.empty((g, 128, n, 4), np.uint8)
        nib[..., 0::2] = words & 0xF
        nib[..., 1::2] = words >> 4
        vals = E2M1[nib]
    vals = vals * np.repeat(np.exp2(scales.astype(np.float64) - 127.0), 8, axis=1)[..., None]
    return vals.transpose(0, 1, 3, 2).reshape(g * 512, n)


B, N, T, D, DV, NQ = 1, 512, 1024, 1024, 256, 256
CAP = 2.0


def setup_inputs():
    n = np.random.standard_normal
    idx = np.sort(np.random.permutation(T)[:B * N].reshape(B, N), axis=1).reshape(-1)
    s = mx_kscale(D)[:, None]
    u = np.ones(T)
    u[idx] = mx_kscale(B * N)
    r = np.random.uniform(0.5, 2.0, T)
    k = n((D, T)) / s
    v = n((DV, T)) / (u * r)
    kp = pack_weight(k, "e2m1")
    return {
        "qT": (n((B, D, NQ)) * s * (0.80 / np.sqrt(D))).astype(np.float32),
        "k_words": np.ascontiguousarray(kp[0].reshape(D // 1024, 2, 128, T, 2).transpose(0, 2, 3, 1, 4)).reshape(D // 1024, 128, T, 4),
        "k_scales": kp[1],
        "vT": v.astype(np.float32),
        "vs": np.tile(u * r, (128, 1)).astype(np.float32),
        "offs": striped(idx),
    }


def reference(qT, k_words, k_scales, vT, vs, offs):
    idx = unstriped(offs)
    k = unpack_weight(k_words.reshape(D // 1024, 128, T, 2, 2).transpose(0, 3, 1, 2, 4).reshape(D // 512, 128, 2 * T), k_scales, "e2m1")
    v = f64(vT)
    pick = lambda x: x[:, idx].reshape(x.shape[0], B, N).transpose(1, 0, 2)
    q = f64(qT)
    score = mxq(q, 1, "e4m3").transpose(0, 2, 1) @ pick(k)
    score = CAP * np.tanh(score / CAP)
    m = score.max(-1, keepdims=True)
    p = np.exp(score - m)
    total = p.sum(-1, keepdims=True)
    w = p * pick(f64(vs))[:, :1, :]
    y = mxq(w, 2, "e4m3") @ mxq(pick(v).transpose(0, 2, 1), 1, "e4m3")
    y = y / total
    return y

@@ -1,0 +1,180 @@
+from contextlib import ExitStack
+
+import concourse.mybir as mybir
+from concourse.masks import make_identity
+
+NQ, SLOTS, TOKENS, D, DV = 256, 512, 1024, 1024, 256
+CAP = 2.0
+FLOPS = 2 * NQ * SLOTS * (D + DV)
+
+F32 = mybir.dt.float32
+BF16 = mybir.dt.bfloat16
+I32 = mybir.dt.int32
+U32 = mybir.dt.uint32
+U16 = mybir.dt.uint16
+U8 = mybir.dt.uint8
+FP8X4 = mybir.dt.float8_e4m3fn_x4
+FP4X4 = mybir.dt.float4_e2m1fn_x4
+ACT = mybir.ActivationFunctionType
+ALU = mybir.AluOpType
+
+P = 128
+PACK = 4
+K_PASS = P * PACK
+PASSES = D // K_PASS
+Q_BLOCKS = NQ // P
+V_BLOCKS = DV // P
+QUADRANTS = 4
+
+
+def tile_attend_cap_srt_kernel(tc, qT, k_words, k_scales, vT, vs, offs, out):
+    nc = tc.nc
+    with ExitStack() as ctx:
+        sb = ctx.enter_context(tc.tile_pool(name="sb", bufs=1))
+        ps = ctx.enter_context(tc.psum_pool(name="ps", bufs=1))
+
+        offsets = sb.tile([P, SLOTS // 16], U16, name="offsets")
+        nc.sync.dma_start(offsets[:], offs)
+
+        scale_pool = sb.tile([P, PASSES, TOKENS // 4], I32, name="scale_pool")
+        nc.vector.memset(scale_pool[:], 0)
+        for quad in range(QUADRANTS):
+            nc.scalar.dma_start(
+                scale_pool[32 * quad : 32 * quad + 4, :, :],
+                k_scales[:, 4 * quad : 4 * quad + 4, :].rearrange("o f t -> f o t").bitcast(I32),
+            )
+
+        vs_pool = sb.tile([P, TOKENS], F32, name="vs_pool")
+        nc.vector.memset(vs_pool[:], 0.0)
+        nc.scalar.dma_start(vs_pool[0:1, :], vs[0:1, :])
+
+        key_pool = sb.tile([P, TOKENS], I32, name="key_pool")
+        nc.sync.dma_start(key_pool[:], k_words[0].rearrange("p t b -> p (t b)").bitcast(I32))
+
+        q_raw = []
+        for o in range(PASSES):
+            t = sb.tile([P, PACK, NQ], F32, name=f"q_raw{o}")
+            nc.sync.dma_start(t[:], qT[0, o * K_PASS : (o + 1) * K_PASS, :].rearrange("(p j) w -> p j w", j=PACK))
+            q_raw.append(t)
+        v_pool = []
+        for h in range(V_BLOCKS):
+            t = sb.tile([P, TOKENS], F32, name=f"v_pool{h}")
+            nc.sync.dma_start(t[:], vT[h * P : (h + 1) * P, :])
+            v_pool.append(t)
+
+        ident = sb.tile([P, P], F32, name="ident")
+        make_identity(nc, ident[:])
+        warm = sb.tile([P, 1], F32, name="warm")
+        nc.scalar.activation(warm[:], ident[:, 0:1], ACT.Exp)
+
+        key_words, key_scales = [], []
+        for o in range(PASSES):
+            t = sb.tile([P, SLOTS], U8, name=f"key_scales{o}", align_bytes=64)
+            nc.vector.tensor_copy(t[:], scale_pool[:, o, :].bitcast(U8).indirect(offsets[:]))
+            key_scales.append(t)
+
+        vs_slots = sb.tile([P, SLOTS], F32, name="vs_slots")
+        nc.vector.tensor_copy(vs_slots[:], vs_pool[:].indirect(offsets[:]))
+        vs_turned = ps.tile([P, PACK, P], F32, name="vs_turned", tag="vs_then_y")
+        for t in range(PACK):
+            nc.tensor.transpose(vs_turned[:, t, :], vs_slots[:, t::PACK], ident[:])
+        vs_cols = sb.tile([P, 1, PACK], F32, name="vs_cols")
+        nc.scalar.copy(vs_cols[:], vs_turned[:, :, 0:1].rearrange("p t c -> p c t"))
+
+        key_pairs = sb.tile([P, SLOTS], U32, name="key_pairs")
+        nc.vector.tensor_copy(key_pairs[:], key_pool[:].bitcast(U32).indirect(offsets[:]))
+        halves = key_pairs[:].bitcast(U16).rearrange("p (n h) -> p h n", h=2)
+        for o in range(PASSES):
+            t = sb.tile([P, 2 * SLOTS], U8, name=f"key_words{o}", align_bytes=64)
+            nc.vector.tensor_copy(t[:].bitcast(U16), halves[:, o, :])
+            key_words.append(t)
+
+        q_codes, q_scales = {}, {}
+        for o in range(PASSES):
+            for b in range(Q_BLOCKS):
+                grouped = sb.tile([P, P, PACK], BF16, name=f"q_grouped{o}{b}", align_bytes=64)
+                dst = grouped[:].rearrange("p (c i) t -> p c t i", i=4)
+                src = q_raw[o][:, :, b * P : (b + 1) * P].rearrange("p t (c i) -> p c t i", i=4)
+                if o == PASSES - 1 and b == 0:
+                    nc.vector.tensor_copy(dst, src)
+                else:
+                    nc.scalar.copy(dst, src)
+                q_codes[o, b] = sb.tile([P, P], U32, name=f"q_codes{o}{b}", align_bytes=64)
+                q_scales[o, b] = sb.tile([P, P], U8, name=f"q_scales{o}{b}", align_bytes=64)
+                nc.vector.quantize_mx(
+                    out=q_codes[o, b][:].bitcast(FP8X4),
+                    scales=q_scales[o, b][:],
+                    in_=grouped[:].rearrange("p c t -> p (c t)"),
+                )
+
+        scores = [ps.tile([P, SLOTS], F32, name=f"scores{b}") for b in range(Q_BLOCKS)]
+        for o in range(PASSES):
+            for b in range(Q_BLOCKS):
+                nc.tensor.matmul_mx(
+                    out=scores[b][:],
+                    lhsT=q_codes[o, b][:].bitcast(FP8X4),
+                    lhsT_scale=q_scales[o, b][:],
+                    rhs=key_words[o][:].bitcast(FP4X4),
+                    rhs_scale=key_scales[o][:],
+                    start=(o == 0),
+                    stop=(o == PASSES - 1),
+                )
+
+        capped, neg_max, probs, total = [], [], [], []
+        for b in range(Q_BLOCKS):
+            c = sb.tile([P, PACK, P], F32, name=f"capped{b}")
+            nc.scalar.activation(c[:], scores[b][:].rearrange("q (s t) -> q t s", t=PACK), ACT.Tanh, scale=1.0 / CAP)
+            capped.append(c)
+            m = sb.tile([P, 1], F32, name=f"neg_max{b}")
+            negated = sb.tile([P, PACK, P], F32, name=f"negated{b}")
+            nc.vector.tensor_scalar(negated[:], c[:], -CAP, None, op0=ALU.mult, op1=ALU.min, accum_out=m[:])
+            neg_max.append(m)
+        for b in range(Q_BLOCKS):
+            pr = sb.tile([P, PACK, P], F32, name=f"probs{b}")
+            l = sb.tile([P, 1], F32, name=f"total{b}")
+            nc.scalar.activation(pr[:], capped[b][:], ACT.Exp, bias=neg_max[b][:], scale=CAP, accum_out=l[:])
+            probs.append(pr)
+            total.append(l)
+
+        v_grouped = sb.tile([P, DV, PACK], BF16, name="v_grouped", align_bytes=64)
+        for h in range(V_BLOCKS):
+            g = sb.tile([P, SLOTS], F32, name=f"v_slots{h}")
+            nc.vector.tensor_copy(g[:], v_pool[h][:].indirect(offsets[:]))
+            turned = ps.tile([P, PACK, P], F32, name=f"v_turned{h}")
+            for t in range(PACK):
+                nc.tensor.transpose(turned[:, t, :], g[:, t::PACK], ident[:])
+            nc.scalar.copy(v_grouped[:, h * P : (h + 1) * P, :], turned[:].rearrange("s t e -> s e t"))
+        v_codes = sb.tile([P, DV], U32, name="v_codes", align_bytes=64)
+        v_scales = sb.tile([P, DV], U8, name="v_scales", align_bytes=64)
+        nc.vector.quantize_mx(
+            out=v_codes[:].bitcast(FP8X4), scales=v_scales[:], in_=v_grouped[:].rearrange("s e t -> s (e t)")
+        )
+
+        for b in range(Q_BLOCKS):
+            turned = ps.tile([P, PACK, P], F32, name=f"p_turned{b}")
+            for t in range(PACK):
+                nc.tensor.transpose(turned[:, t, :], probs[b][:, t, :], ident[:])
+            w = sb.tile([P, P, PACK], BF16, name=f"w_grouped{b}", align_bytes=64)
+            nc.vector.tensor_tensor(
+                w[:], turned[:].rearrange("s t q -> s q t"), vs_cols[:].to_broadcast([P, P, PACK]), ALU.mult
+            )
+            w_codes = sb.tile([P, P], U32, name=f"w_codes{b}", align_bytes=64)
+            w_scales = sb.tile([P, P], U8, name=f"w_scales{b}", align_bytes=64)
+            nc.vector.quantize_mx(
+                out=w_codes[:].bitcast(FP8X4), scales=w_scales[:], in_=w[:].rearrange("s q t -> s (q t)")
+            )
+            inv = sb.tile([P, 1], F32, name=f"inv{b}")
+            nc.vector.reciprocal(inv[:], total[b][:])
+            y = ps.tile([P, DV], F32, name=f"y{b}", tag="vs_then_y" if b == 0 else "y_last")
+            nc.tensor.matmul_mx(
+                out=y[:],
+                lhsT=w_codes[:].bitcast(FP8X4),
+                lhsT_scale=w_scales[:],
+                rhs=v_codes[:].bitcast(FP8X4),
+                rhs_scale=v_scales[:],
+                start=True,
+                stop=True,
+            )
+            res = sb.tile([P, DV], F32, name=f"res{b}")
+            nc.scalar.activation(res[:], y[:], ACT.Copy, scale=inv[:])
+            nc.sync.dma_start(out[0, b * P : (b + 1) * P, :], res[:])

@@ -27,6 +27,16 @@ V_BLOCKS = DV // P
 QUADRANTS = 4
 
 
+def quantize(nc, sb, grouped, name, tag=None):
+    width = grouped.shape[1]
+    codes = sb.tile([P, width], U32, name=name + "_codes", tag=tag or name + "_codes", align_bytes=64)
+    scales = sb.tile([P, width], U8, name=name + "_scales", align_bytes=64)
+    nc.vector.quantize_mx(
+        out=codes[:].bitcast(FP8X4), scales=scales[:], in_=grouped[:].rearrange("p c t -> p (c t)")
+    )
+    return codes, scales
+
+
 def tile_attend_cap_srt_kernel(tc, qT, k_words, k_scales, vT, vs, offs, out):
     nc = tc.nc
     with ExitStack() as ctx:
@@ -36,26 +46,26 @@ def tile_attend_cap_srt_kernel(tc, qT, k_words, k_scales, vT, vs, offs, out):
         offsets = sb.tile([P, SLOTS // 16], U16, name="offsets")
         nc.sync.dma_start(offsets[:], offs)
 
+        key_pool = sb.tile([P, TOKENS], I32, name="key_pool")
+        nc.sync.dma_start(key_pool[:], k_words[0].rearrange("p t b -> p (t b)").bitcast(I32))
+
         scale_pool = sb.tile([P, PASSES, TOKENS // 4], I32, name="scale_pool")
         nc.vector.memset(scale_pool[:], 0)
         for quad in range(QUADRANTS):
-            nc.scalar.dma_start(
+            nc.sync.dma_start(
                 scale_pool[32 * quad : 32 * quad + 4, :, :],
                 k_scales[:, 4 * quad : 4 * quad + 4, :].rearrange("o f t -> f o t").bitcast(I32),
             )
 
         vs_pool = sb.tile([P, TOKENS], F32, name="vs_pool")
         nc.vector.memset(vs_pool[:], 0.0)
-        nc.scalar.dma_start(vs_pool[0:1, :], vs[0:1, :])
-
-        key_pool = sb.tile([P, TOKENS], I32, name="key_pool")
-        nc.sync.dma_start(key_pool[:], k_words[0].rearrange("p t b -> p (t b)").bitcast(I32))
-
         q_raw = []
         for o in range(PASSES):
             t = sb.tile([P, PACK, NQ], F32, name=f"q_raw{o}")
             nc.sync.dma_start(t[:], qT[0, o * K_PASS : (o + 1) * K_PASS, :].rearrange("(p j) w -> p j w", j=PACK))
             q_raw.append(t)
+            if o == 0:
+                nc.sync.dma_start(vs_pool[0:1, :], vs[0:1, :])
         v_pool = []
         for h in range(V_BLOCKS):
             t = sb.tile([P, TOKENS], F32, name=f"v_pool{h}")
@@ -67,114 +77,118 @@ def tile_attend_cap_srt_kernel(tc, qT, k_words, k_scales, vT, vs, offs, out):
         warm = sb.tile([P, 1], F32, name="warm")
         nc.scalar.activation(warm[:], ident[:, 0:1], ACT.Exp)
 
-        key_words, key_scales = [], []
-        for o in range(PASSES):
-            t = sb.tile([P, SLOTS], U8, name=f"key_scales{o}", align_bytes=64)
-            nc.vector.tensor_copy(t[:], scale_pool[:, o, :].bitcast(U8).indirect(offsets[:]))
-            key_scales.append(t)
-
-        vs_slots = sb.tile([P, SLOTS], F32, name="vs_slots")
-        nc.vector.tensor_copy(vs_slots[:], vs_pool[:].indirect(offsets[:]))
-        vs_turned = ps.tile([P, PACK, P], F32, name="vs_turned", tag="vs_then_y")
-        for t in range(PACK):
-            nc.tensor.transpose(vs_turned[:, t, :], vs_slots[:, t::PACK], ident[:])
-        vs_cols = sb.tile([P, 1, PACK], F32, name="vs_cols")
-        nc.scalar.copy(vs_cols[:], vs_turned[:, :, 0:1].rearrange("p t c -> p c t"))
-
         key_pairs = sb.tile([P, SLOTS], U32, name="key_pairs")
         nc.vector.tensor_copy(key_pairs[:], key_pool[:].bitcast(U32).indirect(offsets[:]))
+        key_words, key_scales = [], []
         halves = key_pairs[:].bitcast(U16).rearrange("p (n h) -> p h n", h=2)
         for o in range(PASSES):
             t = sb.tile([P, 2 * SLOTS], U8, name=f"key_words{o}", align_bytes=64)
             nc.vector.tensor_copy(t[:].bitcast(U16), halves[:, o, :])
             key_words.append(t)
-
-        q_codes, q_scales = {}, {}
         for o in range(PASSES):
+            t = sb.tile([P, SLOTS], U8, name=f"key_scales{o}", align_bytes=64)
+            nc.vector.tensor_copy(t[:], scale_pool[:, o, :].bitcast(U8).indirect(offsets[:]))
+            key_scales.append(t)
+
+        scores = [ps.tile([P, SLOTS], F32, name=f"scores{b}", tag=f"bank{b}") for b in range(Q_BLOCKS)]
+
+        def score_pass(o):
             for b in range(Q_BLOCKS):
-                grouped = sb.tile([P, P, PACK], BF16, name=f"q_grouped{o}{b}", align_bytes=64)
-                dst = grouped[:].rearrange("p (c i) t -> p c t i", i=4)
-                src = q_raw[o][:, :, b * P : (b + 1) * P].rearrange("p t (c i) -> p c t i", i=4)
-                if o == PASSES - 1 and b == 0:
-                    nc.vector.tensor_copy(dst, src)
-                else:
-                    nc.scalar.copy(dst, src)
-                q_codes[o, b] = sb.tile([P, P], U32, name=f"q_codes{o}{b}", align_bytes=64)
-                q_scales[o, b] = sb.tile([P, P], U8, name=f"q_scales{o}{b}", align_bytes=64)
-                nc.vector.quantize_mx(
-                    out=q_codes[o, b][:].bitcast(FP8X4),
-                    scales=q_scales[o, b][:],
-                    in_=grouped[:].rearrange("p c t -> p (c t)"),
+                grouped = sb.tile([P, P, PACK], BF16, name=f"q_grouped{o}{b}", tag=f"q_grouped{o}{b}", align_bytes=64)
+                nc.scalar.copy(
+                    grouped[:].rearrange("p (c i) t -> p c t i", i=4),
+                    q_raw[o][:, :, b * P : (b + 1) * P].rearrange("p t (c i) -> p c t i", i=4),
                 )
-
-        scores = [ps.tile([P, SLOTS], F32, name=f"scores{b}") for b in range(Q_BLOCKS)]
-        for o in range(PASSES):
-            for b in range(Q_BLOCKS):
+                codes, scales = quantize(nc, sb, grouped, f"q{o}{b}")
                 nc.tensor.matmul_mx(
                     out=scores[b][:],
-                    lhsT=q_codes[o, b][:].bitcast(FP8X4),
-                    lhsT_scale=q_scales[o, b][:],
+                    lhsT=codes[:].bitcast(FP8X4),
+                    lhsT_scale=scales[:],
                     rhs=key_words[o][:].bitcast(FP4X4),
                     rhs_scale=key_scales[o][:],
                     start=(o == 0),
                     stop=(o == PASSES - 1),
                 )
 
-        capped, neg_max, probs, total = [], [], [], []
-        for b in range(Q_BLOCKS):
-            c = sb.tile([P, PACK, P], F32, name=f"capped{b}")
-            nc.scalar.activation(c[:], scores[b][:].rearrange("q (s t) -> q t s", t=PACK), ACT.Tanh, scale=1.0 / CAP)
-            capped.append(c)
-            m = sb.tile([P, 1], F32, name=f"neg_max{b}")
-            negated = sb.tile([P, PACK, P], F32, name=f"negated{b}")
-            nc.vector.tensor_scalar(negated[:], c[:], -CAP, None, op0=ALU.mult, op1=ALU.min, accum_out=m[:])
-            neg_max.append(m)
-        for b in range(Q_BLOCKS):
-            pr = sb.tile([P, PACK, P], F32, name=f"probs{b}")
-            l = sb.tile([P, 1], F32, name=f"total{b}")
-            nc.scalar.activation(pr[:], capped[b][:], ACT.Exp, bias=neg_max[b][:], scale=CAP, accum_out=l[:])
-            probs.append(pr)
-            total.append(l)
+        score_pass(0)
 
-        v_grouped = sb.tile([P, DV, PACK], BF16, name="v_grouped", align_bytes=64)
-        for h in range(V_BLOCKS):
-            g = sb.tile([P, SLOTS], F32, name=f"v_slots{h}")
+        vs_slots = sb.tile([P, SLOTS], F32, name="vs_slots", tag="q_grouped01", align_bytes=64)
+        nc.vector.tensor_copy(vs_slots[:], vs_pool[:].indirect(offsets[:]))
+
+        score_pass(1)
+
+        vs_turned = ps.tile([P, PACK, P], F32, name="vs_turned", tag="bank2")
+        for t in range(PACK):
+            nc.tensor.transpose(vs_turned[:, t, :], vs_slots[:, t::PACK], ident[:])
+
+        def gather_values(h, tag):
+            g = sb.tile([P, SLOTS], F32, name=f"v_slots{h}", tag=tag, align_bytes=64)
             nc.vector.tensor_copy(g[:], v_pool[h][:].indirect(offsets[:]))
             turned = ps.tile([P, PACK, P], F32, name=f"v_turned{h}")
             for t in range(PACK):
                 nc.tensor.transpose(turned[:, t, :], g[:, t::PACK], ident[:])
-            nc.scalar.copy(v_grouped[:, h * P : (h + 1) * P, :], turned[:].rearrange("s t e -> s e t"))
-        v_codes = sb.tile([P, DV], U32, name="v_codes", align_bytes=64)
-        v_scales = sb.tile([P, DV], U8, name="v_scales", align_bytes=64)
-        nc.vector.quantize_mx(
-            out=v_codes[:].bitcast(FP8X4), scales=v_scales[:], in_=v_grouped[:].rearrange("s e t -> s (e t)")
-        )
+            return turned
 
+        v_turned = [gather_values(0, "q_grouped11")]
+
+        capped, neg_max, probs, total = [], [], [], []
         for b in range(Q_BLOCKS):
+            c = sb.tile([P, PACK, P], F32, name=f"capped{b}", tag=f"capped{b}", align_bytes=64)
+            nc.scalar.activation(c[:], scores[b][:].rearrange("q (s t) -> q t s", t=PACK), ACT.Tanh, scale=1.0 / CAP)
+            capped.append(c)
+            m = sb.tile([P, 1], F32, name=f"neg_max{b}")
+            negated = sb.tile([P, PACK, P], F32, name=f"negated{b}", tag=f"negated{b}", align_bytes=64)
+            nc.vector.tensor_scalar(negated[:], c[:], -CAP, None, op0=ALU.mult, op1=ALU.min, accum_out=m[:])
+            neg_max.append(m)
+        p_turned = []
+        for b in range(Q_BLOCKS):
+            pr = sb.tile([P, PACK, P], F32, name=f"probs{b}")
+            l = sb.tile([P, 1], F32, name=f"total{b}")
+            nc.scalar.activation(pr[:], capped[b][:], ACT.Exp, bias=neg_max[b][:], scale=CAP, accum_out=l[:])
+            total.append(l)
             turned = ps.tile([P, PACK, P], F32, name=f"p_turned{b}")
             for t in range(PACK):
-                nc.tensor.transpose(turned[:, t, :], probs[b][:, t, :], ident[:])
+                nc.tensor.transpose(turned[:, t, :], pr[:, t, :], ident[:])
+            p_turned.append(turned)
+            if b == 0:
+                vs_cols = sb.tile([P, 1, PACK], F32, name="vs_cols", tag="vs_cols", align_bytes=64)
+                nc.scalar.copy(vs_cols[:], vs_turned[:, :, 0:1].rearrange("p t c -> p c t"))
+
+        v_turned.append(gather_values(1, "negated1"))
+
+        w_grouped, inv = [], []
+        for b in range(Q_BLOCKS):
             w = sb.tile([P, P, PACK], BF16, name=f"w_grouped{b}", align_bytes=64)
             nc.vector.tensor_tensor(
-                w[:], turned[:].rearrange("s t q -> s q t"), vs_cols[:].to_broadcast([P, P, PACK]), ALU.mult
+                w[:], p_turned[b][:].rearrange("s t q -> s q t"), vs_cols[:].to_broadcast([P, P, PACK]), ALU.mult
             )
-            w_codes = sb.tile([P, P], U32, name=f"w_codes{b}", align_bytes=64)
-            w_scales = sb.tile([P, P], U8, name=f"w_scales{b}", align_bytes=64)
-            nc.vector.quantize_mx(
-                out=w_codes[:].bitcast(FP8X4), scales=w_scales[:], in_=w[:].rearrange("s q t -> s (q t)")
-            )
-            inv = sb.tile([P, 1], F32, name=f"inv{b}")
-            nc.vector.reciprocal(inv[:], total[b][:])
-            y = ps.tile([P, DV], F32, name=f"y{b}", tag="vs_then_y" if b == 0 else "y_last")
-            nc.tensor.matmul_mx(
-                out=y[:],
-                lhsT=w_codes[:].bitcast(FP8X4),
-                lhsT_scale=w_scales[:],
-                rhs=v_codes[:].bitcast(FP8X4),
-                rhs_scale=v_scales[:],
-                start=True,
-                stop=True,
-            )
-            res = sb.tile([P, DV], F32, name=f"res{b}")
-            nc.scalar.activation(res[:], y[:], ACT.Copy, scale=inv[:])
-            nc.sync.dma_start(out[0, b * P : (b + 1) * P, :], res[:])
+            w_grouped.append(w)
+            r = sb.tile([P, 1], F32, name=f"inv{b}")
+            nc.vector.reciprocal(r[:], total[b][:])
+            inv.append(r)
+
+        weights = [quantize(nc, sb, w_grouped[0], "w0", tag="vs_cols")]
+        y_banks = {(0, 0): "bank2", (1, 0): "bank0", (0, 1): "bank1", (1, 1): "bank3"}
+        for h in range(V_BLOCKS):
+            grouped = sb.tile([P, P, PACK], BF16, name=f"v_grouped{h}", tag=f"capped{1 - h}", align_bytes=64)
+            nc.scalar.copy(grouped[:], v_turned[h][:].rearrange("s t e -> s e t"))
+            v_codes, v_scales = quantize(nc, sb, grouped, f"v{h}")
+            if h == 0:
+                weights.append(quantize(nc, sb, w_grouped[1], "w1"))
+            for b in range(Q_BLOCKS):
+                y = ps.tile([P, P], F32, name=f"y{b}{h}", tag=y_banks[b, h])
+                nc.tensor.matmul_mx(
+                    out=y[:],
+                    lhsT=weights[b][0][:].bitcast(FP8X4),
+                    lhsT_scale=weights[b][1][:],
+                    rhs=v_codes[:].bitcast(FP8X4),
+                    rhs_scale=v_scales[:],
+                    start=True,
+                    stop=True,
+                )
+                res = sb.tile([P, P], F32, name=f"res{b}{h}")
+                if b == 1:
+                    nc.vector.tensor_scalar(res[:], y[:], inv[b][:], None, op0=ALU.mult)
+                else:
+                    nc.scalar.activation(res[:], y[:], ACT.Copy, scale=inv[b][:])
+                nc.sync.dma_start(out[0, b * P : (b + 1) * P, h * P : (h + 1) * P], res[:])

@@ -43,6 +43,9 @@ def tile_attend_cap_srt_kernel(tc, qT, k_words, k_scales, vT, vs, offs, out):
         sb = ctx.enter_context(tc.tile_pool(name="sb", bufs=1))
         ps = ctx.enter_context(tc.psum_pool(name="ps", bufs=1))
 
+        vs_pool = sb.tile([P, TOKENS], F32, name="vs_pool")
+        nc.scalar.dma_start(vs_pool[P - 1 : P, :], vs[0:1, :])
+
         offsets = sb.tile([P, SLOTS // 16], U16, name="offsets")
         nc.sync.dma_start(offsets[:], offs)
 
@@ -51,21 +54,18 @@ def tile_attend_cap_srt_kernel(tc, qT, k_words, k_scales, vT, vs, offs, out):
 
         scale_pool = sb.tile([P, PASSES, TOKENS // 4], I32, name="scale_pool")
         nc.vector.memset(scale_pool[:], 0)
+        nc.vector.memset(vs_pool[0 : P - 1, :], 0.0)
         for quad in range(QUADRANTS):
             nc.sync.dma_start(
                 scale_pool[32 * quad : 32 * quad + 4, :, :],
                 k_scales[:, 4 * quad : 4 * quad + 4, :].rearrange("o f t -> f o t").bitcast(I32),
             )
 
-        vs_pool = sb.tile([P, TOKENS], F32, name="vs_pool")
-        nc.vector.memset(vs_pool[:], 0.0)
         q_raw = []
         for o in range(PASSES):
             t = sb.tile([P, PACK, NQ], F32, name=f"q_raw{o}")
             nc.sync.dma_start(t[:], qT[0, o * K_PASS : (o + 1) * K_PASS, :].rearrange("(p j) w -> p j w", j=PACK))
             q_raw.append(t)
-            if o == 0:
-                nc.sync.dma_start(vs_pool[0:1, :], vs[0:1, :])
         v_pool = []
         for h in range(V_BLOCKS):
             t = sb.tile([P, TOKENS], F32, name=f"v_pool{h}")
@@ -74,25 +74,28 @@ def tile_attend_cap_srt_kernel(tc, qT, k_words, k_scales, vT, vs, offs, out):
 
         ident = sb.tile([P, P], F32, name="ident")
         make_identity(nc, ident[:])
-        warm = sb.tile([P, 1], F32, name="warm")
-        nc.scalar.activation(warm[:], ident[:, 0:1], ACT.Exp)
+
+        vs_slots = sb.tile([P, SLOTS], F32, name="vs_slots")
+        nc.vector.tensor_copy(vs_slots[:], vs_pool[:].indirect(offsets[:]))
+        vs_turned = ps.tile([P, PACK, P], F32, name="vs_turned", tag="bank2")
+        for t in range(PACK):
+            nc.tensor.transpose(vs_turned[:, t, :], vs_slots[:, t::PACK], ident[:])
+        vs_cols = sb.tile([P, 1, PACK], F32, name="vs_cols", tag="vs_cols", align_bytes=64)
+        nc.scalar.copy(vs_cols[:], vs_turned[:, :, P - 1 : P].rearrange("p t c -> p c t"))
 
         key_pairs = sb.tile([P, SLOTS], U32, name="key_pairs")
         nc.vector.tensor_copy(key_pairs[:], key_pool[:].bitcast(U32).indirect(offsets[:]))
-        key_words, key_scales = [], []
-        halves = key_pairs[:].bitcast(U16).rearrange("p (n h) -> p h n", h=2)
-        for o in range(PASSES):
-            t = sb.tile([P, 2 * SLOTS], U8, name=f"key_words{o}", align_bytes=64)
-            nc.vector.tensor_copy(t[:].bitcast(U16), halves[:, o, :])
-            key_words.append(t)
-        for o in range(PASSES):
-            t = sb.tile([P, SLOTS], U8, name=f"key_scales{o}", align_bytes=64)
-            nc.vector.tensor_copy(t[:], scale_pool[:, o, :].bitcast(U8).indirect(offsets[:]))
-            key_scales.append(t)
+        key_words = sb.tile([P, PASSES, 2 * SLOTS], U8, name="key_words", align_bytes=64)
+        nc.vector.tensor_copy(
+            key_words[:].bitcast(U16), key_pairs[:].bitcast(U16).rearrange("p (n h) -> p h n", h=PASSES)
+        )
 
         scores = [ps.tile([P, SLOTS], F32, name=f"scores{b}", tag=f"bank{b}") for b in range(Q_BLOCKS)]
-
-        def score_pass(o):
+        for o in range(PASSES):
+            key_scales = sb.tile(
+                [P, SLOTS], U8, name=f"key_scales{o}", tag="q_grouped00" if o == 1 else "key_scales0", align_bytes=64
+            )
+            nc.vector.tensor_copy(key_scales[:], scale_pool[:, o, :].bitcast(U8).indirect(offsets[:]))
             for b in range(Q_BLOCKS):
                 grouped = sb.tile([P, P, PACK], BF16, name=f"q_grouped{o}{b}", tag=f"q_grouped{o}{b}", align_bytes=64)
                 nc.scalar.copy(
@@ -104,34 +107,29 @@ def tile_attend_cap_srt_kernel(tc, qT, k_words, k_scales, vT, vs, offs, out):
                     out=scores[b][:],
                     lhsT=codes[:].bitcast(FP8X4),
                     lhsT_scale=scales[:],
-                    rhs=key_words[o][:].bitcast(FP4X4),
-                    rhs_scale=key_scales[o][:],
+                    rhs=key_words[:, o, :].bitcast(FP4X4),
+                    rhs_scale=key_scales[:],
                     start=(o == 0),
                     stop=(o == PASSES - 1),
                 )
 
-        score_pass(0)
-
-        vs_slots = sb.tile([P, SLOTS], F32, name="vs_slots", tag="q_grouped01", align_bytes=64)
-        nc.vector.tensor_copy(vs_slots[:], vs_pool[:].indirect(offsets[:]))
-
-        score_pass(1)
-
-        vs_turned = ps.tile([P, PACK, P], F32, name="vs_turned", tag="bank2")
-        for t in range(PACK):
-            nc.tensor.transpose(vs_turned[:, t, :], vs_slots[:, t::PACK], ident[:])
-
         def gather_values(h, tag):
-            g = sb.tile([P, SLOTS], F32, name=f"v_slots{h}", tag=tag, align_bytes=64)
+            g = sb.tile([P, SLOTS], BF16, name=f"v_slots{h}", tag=tag, align_bytes=64)
             nc.vector.tensor_copy(g[:], v_pool[h][:].indirect(offsets[:]))
-            turned = ps.tile([P, PACK, P], F32, name=f"v_turned{h}")
-            for t in range(PACK):
-                nc.tensor.transpose(turned[:, t, :], g[:, t::PACK], ident[:])
-            return turned
+            return g
 
-        v_turned = [gather_values(0, "q_grouped11")]
+        def turn_values(h, g, tag):
+            turned = ps.tile([P, 2, P], F32, name=f"v_turned{h}", tag="bank0")
+            pairs = g[:].bitcast(F32)
+            for u in range(2):
+                nc.tensor.transpose(turned[:, u, :], pairs[:, u::2], ident[:])
+            grouped = sb.tile([P, P, 2], F32, name=f"v_grouped{h}", tag=tag, align_bytes=64)
+            nc.scalar.copy(grouped[:], turned[:].rearrange("s u e -> s e u"))
+            return grouped
 
-        capped, neg_max, probs, total = [], [], [], []
+        v_slots0 = gather_values(0, "q_grouped10")
+
+        capped, neg_max = [], []
         for b in range(Q_BLOCKS):
             c = sb.tile([P, PACK, P], F32, name=f"capped{b}", tag=f"capped{b}", align_bytes=64)
             nc.scalar.activation(c[:], scores[b][:].rearrange("q (s t) -> q t s", t=PACK), ACT.Tanh, scale=1.0 / CAP)
@@ -140,55 +138,54 @@ def tile_attend_cap_srt_kernel(tc, qT, k_words, k_scales, vT, vs, offs, out):
             negated = sb.tile([P, PACK, P], F32, name=f"negated{b}", tag=f"negated{b}", align_bytes=64)
             nc.vector.tensor_scalar(negated[:], c[:], -CAP, None, op0=ALU.mult, op1=ALU.min, accum_out=m[:])
             neg_max.append(m)
+        total = sb.tile([P, Q_BLOCKS], F32, name="total")
         p_turned = []
         for b in range(Q_BLOCKS):
-            pr = sb.tile([P, PACK, P], F32, name=f"probs{b}")
-            l = sb.tile([P, 1], F32, name=f"total{b}")
-            nc.scalar.activation(pr[:], capped[b][:], ACT.Exp, bias=neg_max[b][:], scale=CAP, accum_out=l[:])
-            total.append(l)
+            pr = sb.tile([P, PACK, P], F32, name=f"probs{b}", tag=f"probs{b}", align_bytes=64)
+            nc.scalar.activation(
+                pr[:], capped[b][:], ACT.Exp, bias=neg_max[b][:], scale=CAP, accum_out=total[:, b : b + 1]
+            )
             turned = ps.tile([P, PACK, P], F32, name=f"p_turned{b}")
             for t in range(PACK):
                 nc.tensor.transpose(turned[:, t, :], pr[:, t, :], ident[:])
             p_turned.append(turned)
-            if b == 0:
-                vs_cols = sb.tile([P, 1, PACK], F32, name="vs_cols", tag="vs_cols", align_bytes=64)
-                nc.scalar.copy(vs_cols[:], vs_turned[:, :, 0:1].rearrange("p t c -> p c t"))
 
-        v_turned.append(gather_values(1, "negated1"))
+        v_slots1 = gather_values(1, "negated1")
+        v_grouped = [turn_values(0, v_slots0, "capped1"), turn_values(1, v_slots1, "v_grouped1")]
 
-        w_grouped, inv = [], []
+        v_codes = sb.tile([P, DV], U32, name="v_codes", align_bytes=64)
+        v_scales = sb.tile([P, DV], U8, name="v_scales", align_bytes=64)
+        inv = sb.tile([P, Q_BLOCKS], F32, name="inv")
+        w_grouped = []
         for b in range(Q_BLOCKS):
             w = sb.tile([P, P, PACK], BF16, name=f"w_grouped{b}", align_bytes=64)
             nc.vector.tensor_tensor(
                 w[:], p_turned[b][:].rearrange("s t q -> s q t"), vs_cols[:].to_broadcast([P, P, PACK]), ALU.mult
             )
             w_grouped.append(w)
-            r = sb.tile([P, 1], F32, name=f"inv{b}")
-            nc.vector.reciprocal(r[:], total[b][:])
-            inv.append(r)
+            if b == 0:
+                nc.vector.reciprocal(inv[:], total[:])
+            nc.vector.quantize_mx(
+                out=v_codes[:, b * P : (b + 1) * P].bitcast(FP8X4),
+                scales=v_scales[:, b * P : (b + 1) * P],
+                in_=v_grouped[b][:].rearrange("s e u -> s (e u)").bitcast(BF16),
+            )
 
-        weights = [quantize(nc, sb, w_grouped[0], "w0", tag="vs_cols")]
-        y_banks = {(0, 0): "bank2", (1, 0): "bank0", (0, 1): "bank1", (1, 1): "bank3"}
-        for h in range(V_BLOCKS):
-            grouped = sb.tile([P, P, PACK], BF16, name=f"v_grouped{h}", tag=f"capped{1 - h}", align_bytes=64)
-            nc.scalar.copy(grouped[:], v_turned[h][:].rearrange("s t e -> s e t"))
-            v_codes, v_scales = quantize(nc, sb, grouped, f"v{h}")
-            if h == 0:
-                weights.append(quantize(nc, sb, w_grouped[1], "w1"))
-            for b in range(Q_BLOCKS):
-                y = ps.tile([P, P], F32, name=f"y{b}{h}", tag=y_banks[b, h])
-                nc.tensor.matmul_mx(
-                    out=y[:],
-                    lhsT=weights[b][0][:].bitcast(FP8X4),
-                    lhsT_scale=weights[b][1][:],
-                    rhs=v_codes[:].bitcast(FP8X4),
-                    rhs_scale=v_scales[:],
-                    start=True,
-                    stop=True,
-                )
-                res = sb.tile([P, P], F32, name=f"res{b}{h}")
-                if b == 1:
-                    nc.vector.tensor_scalar(res[:], y[:], inv[b][:], None, op0=ALU.mult)
-                else:
-                    nc.scalar.activation(res[:], y[:], ACT.Copy, scale=inv[b][:])
-                nc.sync.dma_start(out[0, b * P : (b + 1) * P, h * P : (h + 1) * P], res[:])
+        for b in range(Q_BLOCKS):
+            w_codes, w_scales = quantize(nc, sb, w_grouped[b], f"w{b}", tag="probs1" if b == 0 else None)
+            y = ps.tile([P, DV], F32, name=f"y{b}", tag=f"bank{2 - b}")
+            nc.tensor.matmul_mx(
+                out=y[:],
+                lhsT=w_codes[:].bitcast(FP8X4),
+                lhsT_scale=w_scales[:],
+                rhs=v_codes[:].bitcast(FP8X4),
+                rhs_scale=v_scales[:],
+                start=True,
+                stop=True,
+            )
+            res = sb.tile([P, DV], F32, name=f"res{b}")
+            if b == 1:
+                nc.vector.tensor_scalar(res[:], y[:], inv[:, b : b + 1], None, op0=ALU.mult)
+            else:
+                nc.scalar.activation(res[:], y[:], ACT.Copy, scale=inv[:, b : b + 1])
+            nc.sync.dma_start(out[0, b * P : (b + 1) * P, :], res[:])

@@ -63,12 +63,12 @@ def tile_attend_cap_srt_kernel(tc, qT, k_words, k_scales, vT, vs, offs, out):
 
         q_raw = []
         for o in range(PASSES):
-            t = sb.tile([P, PACK, NQ], F32, name=f"q_raw{o}")
+            t = sb.tile([P, PACK, NQ], F32, name=f"q_raw{o}", tag=f"q_raw{o}", align_bytes=64)
             nc.sync.dma_start(t[:], qT[0, o * K_PASS : (o + 1) * K_PASS, :].rearrange("(p j) w -> p j w", j=PACK))
             q_raw.append(t)
         v_pool = []
         for h in range(V_BLOCKS):
-            t = sb.tile([P, TOKENS], F32, name=f"v_pool{h}")
+            t = sb.tile([P, TOKENS], F32, name=f"v_pool{h}", tag=f"v_pool{h}", align_bytes=64)
             nc.sync.dma_start(t[:], vT[h * P : (h + 1) * P, :])
             v_pool.append(t)
 
@@ -93,7 +93,7 @@ def tile_attend_cap_srt_kernel(tc, qT, k_words, k_scales, vT, vs, offs, out):
         scores = [ps.tile([P, SLOTS], F32, name=f"scores{b}", tag=f"bank{b}") for b in range(Q_BLOCKS)]
         for o in range(PASSES):
             key_scales = sb.tile(
-                [P, SLOTS], U8, name=f"key_scales{o}", tag="q_grouped00" if o == 1 else "key_scales0", align_bytes=64
+                [P, SLOTS], U8, name=f"key_scales{o}", tag="q_raw0" if o == 1 else "key_scales0", align_bytes=64
             )
             nc.vector.tensor_copy(key_scales[:], scale_pool[:, o, :].bitcast(U8).indirect(offsets[:]))
             for b in range(Q_BLOCKS):
@@ -118,16 +118,20 @@ def tile_attend_cap_srt_kernel(tc, qT, k_words, k_scales, vT, vs, offs, out):
             nc.vector.tensor_copy(g[:], v_pool[h][:].indirect(offsets[:]))
             return g
 
-        def turn_values(h, g, tag):
-            turned = ps.tile([P, 2, P], F32, name=f"v_turned{h}", tag="bank0")
+        def turn_values(h, g, copy):
+            turned = ps.tile([P, 2, P], F32, name=f"v_turned{h}", tag=f"bank{h}")
             pairs = g[:].bitcast(F32)
             for u in range(2):
                 nc.tensor.transpose(turned[:, u, :], pairs[:, u::2], ident[:])
-            grouped = sb.tile([P, P, 2], F32, name=f"v_grouped{h}", tag=tag, align_bytes=64)
-            nc.scalar.copy(grouped[:], turned[:].rearrange("s u e -> s e u"))
-            return grouped
+            grouped = sb.tile([P, P, 2], F32, name=f"v_grouped{h}", align_bytes=64)
+            copy(grouped[:], turned[:].rearrange("s u e -> s e u"))
+            nc.vector.quantize_mx(
+                out=v_codes[:, h * P : (h + 1) * P].bitcast(FP8X4),
+                scales=v_scales[:, h * P : (h + 1) * P],
+                in_=grouped[:].rearrange("s e u -> s (e u)").bitcast(BF16),
+            )
 
-        v_slots0 = gather_values(0, "q_grouped10")
+        v_slots = [gather_values(0, "q_raw1"), gather_values(1, "q_grouped11")]
 
         capped, neg_max = [], []
         for b in range(Q_BLOCKS):
@@ -135,26 +139,36 @@ def tile_attend_cap_srt_kernel(tc, qT, k_words, k_scales, vT, vs, offs, out):
             nc.scalar.activation(c[:], scores[b][:].rearrange("q (s t) -> q t s", t=PACK), ACT.Tanh, scale=1.0 / CAP)
             capped.append(c)
             m = sb.tile([P, 1], F32, name=f"neg_max{b}")
-            negated = sb.tile([P, PACK, P], F32, name=f"negated{b}", tag=f"negated{b}", align_bytes=64)
-            nc.vector.tensor_scalar(negated[:], c[:], -CAP, None, op0=ALU.mult, op1=ALU.min, accum_out=m[:])
+            negated = sb.tile([P, SLOTS], F32, name=f"negated{b}", tag=f"v_pool{1 - b}", align_bytes=64)
+            nc.vector.tensor_scalar(
+                negated[:], c[:].rearrange("q t s -> q (t s)"), -CAP, None, op0=ALU.mult, op1=ALU.min, accum_out=m[:]
+            )
             neg_max.append(m)
-        total = sb.tile([P, Q_BLOCKS], F32, name="total")
+        v_codes = sb.tile([P, DV], U32, name="v_codes", tag="v_pool0", align_bytes=64)
+        v_scales = sb.tile([P, DV], U8, name="v_scales", align_bytes=64)
+        turn_values(0, v_slots[0], nc.scalar.copy)
+        turn_values(1, v_slots[1], nc.vector.tensor_copy)
+        total = sb.tile([P, 2, Q_BLOCKS], F32, name="total")
         p_turned = []
         for b in range(Q_BLOCKS):
             pr = sb.tile([P, PACK, P], F32, name=f"probs{b}", tag=f"probs{b}", align_bytes=64)
-            nc.scalar.activation(
-                pr[:], capped[b][:], ACT.Exp, bias=neg_max[b][:], scale=CAP, accum_out=total[:, b : b + 1]
-            )
             turned = ps.tile([P, PACK, P], F32, name=f"p_turned{b}")
-            for t in range(PACK):
-                nc.tensor.transpose(turned[:, t, :], pr[:, t, :], ident[:])
+            parts = 2
+            planes = PACK // parts
+            for part in range(parts):
+                sl = slice(part * planes, (part + 1) * planes)
+                nc.scalar.activation(
+                    pr[:, sl, :],
+                    capped[b][:, sl, :],
+                    ACT.Exp,
+                    bias=neg_max[b][:],
+                    scale=CAP,
+                    accum_out=total[:, part, b : b + 1],
+                )
+                for t in range(part * planes, (part + 1) * planes):
+                    nc.tensor.transpose(turned[:, t, :], pr[:, t, :], ident[:])
             p_turned.append(turned)
 
-        v_slots1 = gather_values(1, "negated1")
-        v_grouped = [turn_values(0, v_slots0, "capped1"), turn_values(1, v_slots1, "v_grouped1")]
-
-        v_codes = sb.tile([P, DV], U32, name="v_codes", align_bytes=64)
-        v_scales = sb.tile([P, DV], U8, name="v_scales", align_bytes=64)
         inv = sb.tile([P, Q_BLOCKS], F32, name="inv")
         w_grouped = []
         for b in range(Q_BLOCKS):
@@ -164,16 +178,13 @@ def tile_attend_cap_srt_kernel(tc, qT, k_words, k_scales, vT, vs, offs, out):
             )
             w_grouped.append(w)
             if b == 0:
-                nc.vector.reciprocal(inv[:], total[:])
-            nc.vector.quantize_mx(
-                out=v_codes[:, b * P : (b + 1) * P].bitcast(FP8X4),
-                scales=v_scales[:, b * P : (b + 1) * P],
-                in_=v_grouped[b][:].rearrange("s e u -> s (e u)").bitcast(BF16),
-            )
+                nc.vector.tensor_tensor(total[:, 0, :], total[:, 0, :], total[:, 1, :], ALU.add)
+            else:
+                nc.vector.reciprocal(inv[:], total[:, 0, :])
 
         for b in range(Q_BLOCKS):
             w_codes, w_scales = quantize(nc, sb, w_grouped[b], f"w{b}", tag="probs1" if b == 0 else None)
-            y = ps.tile([P, DV], F32, name=f"y{b}", tag=f"bank{2 - b}")
+            y = ps.tile([P, DV], F32, name=f"y{b}", tag=f"bank{2 + b}")
             nc.tensor.matmul_mx(
                 out=y[:],
                 lhsT=w_codes[:].bitcast(FP8X4),

@@ -55,10 +55,10 @@ def tile_attend_cap_srt_kernel(tc, qT, k_words, k_scales, vT, vs, offs, out):
         scale_pool = sb.tile([P, PASSES, TOKENS // 4], I32, name="scale_pool")
         nc.vector.memset(scale_pool[:], 0)
         nc.vector.memset(vs_pool[0 : P - 1, :], 0.0)
-        for quad in range(QUADRANTS):
+        for row in range(4):
             nc.sync.dma_start(
-                scale_pool[32 * quad : 32 * quad + 4, :, :],
-                k_scales[:, 4 * quad : 4 * quad + 4, :].rearrange("o f t -> f o t").bitcast(I32),
+                scale_pool[row:P:32, :, :],
+                k_scales[:, row::4, :].rearrange("o f t -> f o t").bitcast(I32),
             )
 
         q_raw = []
@@ -184,19 +184,21 @@ def tile_attend_cap_srt_kernel(tc, qT, k_words, k_scales, vT, vs, offs, out):
 
         for b in range(Q_BLOCKS):
             w_codes, w_scales = quantize(nc, sb, w_grouped[b], f"w{b}", tag="probs1" if b == 0 else None)
-            y = ps.tile([P, DV], F32, name=f"y{b}", tag=f"bank{2 + b}")
-            nc.tensor.matmul_mx(
-                out=y[:],
-                lhsT=w_codes[:].bitcast(FP8X4),
-                lhsT_scale=w_scales[:],
-                rhs=v_codes[:].bitcast(FP8X4),
-                rhs_scale=v_scales[:],
-                start=True,
-                stop=True,
-            )
             res = sb.tile([P, DV], F32, name=f"res{b}")
-            if b == 1:
-                nc.vector.tensor_scalar(res[:], y[:], inv[:, b : b + 1], None, op0=ALU.mult)
-            else:
-                nc.scalar.activation(res[:], y[:], ACT.Copy, scale=inv[:, b : b + 1])
+            for h in range(V_BLOCKS):
+                cols = slice(h * P, (h + 1) * P)
+                y = ps.tile([P, P], F32, name=f"y{b}{h}", tag=f"bank{2 * b + h}")
+                nc.tensor.matmul_mx(
+                    out=y[:],
+                    lhsT=w_codes[:].bitcast(FP8X4),
+                    lhsT_scale=w_scales[:],
+                    rhs=v_codes[:, cols].bitcast(FP8X4),
+                    rhs_scale=v_scales[:, cols],
+                    start=True,
+                    stop=True,
+                )
+                if h == 1:
+                    nc.vector.tensor_scalar(res[:, cols], y[:], inv[:, b : b + 1], None, op0=ALU.mult)
+                else:
+                    nc.scalar.activation(res[:, cols], y[:], ACT.Copy, scale=inv[:, b : b + 1])
             nc.sync.dma_start(out[0, b * P : (b + 1) * P, :], res[:])

@@ -54,6 +54,9 @@ def tile_attend_cap_srt_kernel(tc, qT, k_words, k_scales, vT, vs, offs, out):
 
         scale_pool = sb.tile([P, PASSES, TOKENS // 4], I32, name="scale_pool")
         nc.vector.memset(scale_pool[:], 0)
+        ident = sb.tile([P, P], F32, name="ident")
+        nc.vector.memset(ident[:], 0.0)
+        make_identity(nc, ident[:], nomemset=True)
         nc.vector.memset(vs_pool[0 : P - 1, :], 0.0)
         for row in range(4):
             nc.sync.dma_start(
@@ -72,16 +75,11 @@ def tile_attend_cap_srt_kernel(tc, qT, k_words, k_scales, vT, vs, offs, out):
             nc.sync.dma_start(t[:], vT[h * P : (h + 1) * P, :])
             v_pool.append(t)
 
-        ident = sb.tile([P, P], F32, name="ident")
-        make_identity(nc, ident[:])
-
         vs_slots = sb.tile([P, SLOTS], F32, name="vs_slots")
         nc.vector.tensor_copy(vs_slots[:], vs_pool[:].indirect(offsets[:]))
         vs_turned = ps.tile([P, PACK, P], F32, name="vs_turned", tag="bank2")
         for t in range(PACK):
             nc.tensor.transpose(vs_turned[:, t, :], vs_slots[:, t::PACK], ident[:])
-        vs_cols = sb.tile([P, 1, PACK], F32, name="vs_cols", tag="vs_cols", align_bytes=64)
-        nc.scalar.copy(vs_cols[:], vs_turned[:, :, P - 1 : P].rearrange("p t c -> p c t"))
 
         key_pairs = sb.tile([P, SLOTS], U32, name="key_pairs")
         nc.vector.tensor_copy(key_pairs[:], key_pool[:].bitcast(U32).indirect(offsets[:]))
@@ -132,6 +130,8 @@ def tile_attend_cap_srt_kernel(tc, qT, k_words, k_scales, vT, vs, offs, out):
             )
 
         v_slots = [gather_values(0, "q_raw1"), gather_values(1, "q_grouped11")]
+        vs_cols = sb.tile([P, 1, PACK], F32, name="vs_cols", tag="q_grouped10", align_bytes=64)
+        nc.scalar.copy(vs_cols[:], vs_turned[:, :, P - 1 : P].rearrange("p t c -> p c t"))
 
         capped, neg_max = [], []
         for b in range(Q_BLOCKS):

@@ -79,7 +79,12 @@ def tile_attend_cap_srt_kernel(tc, qT, k_words, k_scales, vT, vs, offs, out):
         nc.vector.tensor_copy(vs_slots[:], vs_pool[:].indirect(offsets[:]))
         vs_turned = ps.tile([P, PACK, P], F32, name="vs_turned", tag="bank2")
         for t in range(PACK):
-            nc.tensor.transpose(vs_turned[:, t, :], vs_slots[:, t::PACK], ident[:])
+            nc.tensor.transpose(vs_turned[:, t, :], vs_slots[:, t * P : (t + 1) * P], ident[:])
+        vs_cols = sb.tile([P, PACK, 1], F32, name="vs_cols")
+        nc.scalar.copy(vs_cols[:], vs_turned[:, :, P - 1 : P])
+        vs_spread = ps.tile([P, SLOTS], F32, name="vs_spread", tag="bank2")
+        for t in range(PACK):
+            nc.tensor.transpose(vs_spread[:, t * P : (t + 1) * P], vs_cols[:, t, :].to_broadcast([P, P]), ident[:])
 
         key_pairs = sb.tile([P, SLOTS], U32, name="key_pairs")
         nc.vector.tensor_copy(key_pairs[:], key_pool[:].bitcast(U32).indirect(offsets[:]))
@@ -116,75 +121,78 @@ def tile_attend_cap_srt_kernel(tc, qT, k_words, k_scales, vT, vs, offs, out):
             nc.vector.tensor_copy(g[:], v_pool[h][:].indirect(offsets[:]))
             return g
 
-        def turn_values(h, g, copy):
-            turned = ps.tile([P, 2, P], F32, name=f"v_turned{h}", tag=f"bank{h}")
-            pairs = g[:].bitcast(F32)
-            for u in range(2):
-                nc.tensor.transpose(turned[:, u, :], pairs[:, u::2], ident[:])
-            grouped = sb.tile([P, P, 2], F32, name=f"v_grouped{h}", align_bytes=64)
-            copy(grouped[:], turned[:].rearrange("s u e -> s e u"))
-            nc.vector.quantize_mx(
-                out=v_codes[:, h * P : (h + 1) * P].bitcast(FP8X4),
-                scales=v_scales[:, h * P : (h + 1) * P],
-                in_=grouped[:].rearrange("s e u -> s (e u)").bitcast(BF16),
-            )
-
         v_slots = [gather_values(0, "q_raw1"), gather_values(1, "q_grouped11")]
-        vs_cols = sb.tile([P, 1, PACK], F32, name="vs_cols", tag="q_grouped10", align_bytes=64)
-        nc.scalar.copy(vs_cols[:], vs_turned[:, :, P - 1 : P].rearrange("p t c -> p c t"))
+        v_turned = ps.tile([P, V_BLOCKS, 2, P], F32, name="v_turned", tag="bank3")
+        for h in range(V_BLOCKS):
+            pairs = v_slots[h][:].bitcast(F32)
+            for u in range(2):
+                nc.tensor.transpose(v_turned[:, h, u, :], pairs[:, u::2], ident[:])
 
         capped, neg_max = [], []
         for b in range(Q_BLOCKS):
-            c = sb.tile([P, PACK, P], F32, name=f"capped{b}", tag=f"capped{b}", align_bytes=64)
-            nc.scalar.activation(c[:], scores[b][:].rearrange("q (s t) -> q t s", t=PACK), ACT.Tanh, scale=1.0 / CAP)
+            c = sb.tile([P, 2, P, 2], F32, name=f"capped{b}", tag=f"capped{b}", align_bytes=64)
+            nc.scalar.activation(
+                c[:], scores[b][:].rearrange("q (s u e) -> q u s e", u=2, e=2), ACT.Tanh, scale=1.0 / CAP
+            )
             capped.append(c)
             m = sb.tile([P, 1], F32, name=f"neg_max{b}")
             negated = sb.tile([P, SLOTS], F32, name=f"negated{b}", tag=f"v_pool{1 - b}", align_bytes=64)
             nc.vector.tensor_scalar(
-                negated[:], c[:].rearrange("q t s -> q (t s)"), -CAP, None, op0=ALU.mult, op1=ALU.min, accum_out=m[:]
+                negated[:], c[:].rearrange("q u s e -> q (u s e)"), -CAP, None, op0=ALU.mult, op1=ALU.min, accum_out=m[:]
             )
             neg_max.append(m)
-        v_codes = sb.tile([P, DV], U32, name="v_codes", tag="v_pool0", align_bytes=64)
-        v_scales = sb.tile([P, DV], U8, name="v_scales", align_bytes=64)
-        turn_values(0, v_slots[0], nc.scalar.copy)
-        turn_values(1, v_slots[1], nc.vector.tensor_copy)
         total = sb.tile([P, 2, Q_BLOCKS], F32, name="total")
-        p_turned = []
+        vs_halves = vs_spread[:].rearrange("q (s u e) -> q u s e", u=2, e=2)
+        w_turned = []
         for b in range(Q_BLOCKS):
-            pr = sb.tile([P, PACK, P], F32, name=f"probs{b}", tag=f"probs{b}", align_bytes=64)
-            turned = ps.tile([P, PACK, P], F32, name=f"p_turned{b}")
-            parts = 2
-            planes = PACK // parts
-            for part in range(parts):
-                sl = slice(part * planes, (part + 1) * planes)
+            pr = sb.tile([P, 2, P, 2], F32, name=f"probs{b}", align_bytes=64)
+            w = sb.tile([P, 2, P, 2], BF16, name=f"w{b}", align_bytes=64)
+            turned = ps.tile([P, 2, P], F32, name=f"w_turned{b}")
+            for u in range(2):
                 nc.scalar.activation(
-                    pr[:, sl, :],
-                    capped[b][:, sl, :],
+                    pr[:, u],
+                    capped[b][:, u],
                     ACT.Exp,
                     bias=neg_max[b][:],
                     scale=CAP,
-                    accum_out=total[:, part, b : b + 1],
+                    accum_out=total[:, u, b : b + 1],
                 )
-                for t in range(part * planes, (part + 1) * planes):
-                    nc.tensor.transpose(turned[:, t, :], pr[:, t, :], ident[:])
-            p_turned.append(turned)
+                nc.vector.tensor_tensor(w[:, u], pr[:, u], vs_halves[:, u], ALU.mult)
+                nc.tensor.transpose(turned[:, u, :], w[:, u].rearrange("q s e -> q (s e)").bitcast(F32), ident[:])
+            w_turned.append(turned)
 
         inv = sb.tile([P, Q_BLOCKS], F32, name="inv")
+        nc.vector.tensor_tensor(total[:, 0, :], total[:, 0, :], total[:, 1, :], ALU.add)
         w_grouped = []
         for b in range(Q_BLOCKS):
-            w = sb.tile([P, P, PACK], BF16, name=f"w_grouped{b}", align_bytes=64)
-            nc.vector.tensor_tensor(
-                w[:], p_turned[b][:].rearrange("s t q -> s q t"), vs_cols[:].to_broadcast([P, P, PACK]), ALU.mult
+            w_grouped.append(sb.tile([P, P, 2], F32, name=f"w_grouped{b}", tag=f"w_grouped{b}", align_bytes=64))
+        nc.vector.tensor_copy(w_grouped[0][:], w_turned[0][:].rearrange("s u q -> s q u"))
+        v_grouped = sb.tile([P, V_BLOCKS, P, 2], F32, name="v_grouped", tag="capped0", align_bytes=64)
+        nc.scalar.copy(v_grouped[:], v_turned[:].rearrange("s h u e -> s h e u"))
+        v_codes = sb.tile([P, DV], U32, name="v_codes", align_bytes=64)
+        v_scales = sb.tile([P, DV], U8, name="v_scales", align_bytes=64)
+        nc.vector.quantize_mx(
+            out=v_codes[:].bitcast(FP8X4),
+            scales=v_scales[:],
+            in_=v_grouped[:].rearrange("s h e u -> s (h e u)").bitcast(BF16),
+        )
+        nc.vector.reciprocal(inv[:], total[:, 0, :])
+
+        w_quantized = []
+        for b in range(Q_BLOCKS):
+            grouped = w_grouped[b]
+            if b == 1:
+                nc.scalar.copy(grouped[:], w_turned[b][:].rearrange("s u q -> s q u"))
+            codes = sb.tile([P, P], U32, name=f"w_codes{b}", align_bytes=64)
+            scales = sb.tile([P, P], U8, name=f"w_scales{b}", align_bytes=64)
+            nc.vector.quantize_mx(
+                out=codes[:].bitcast(FP8X4), scales=scales[:], in_=grouped[:].rearrange("s q u -> s (q u)").bitcast(BF16)
             )
-            w_grouped.append(w)
-            if b == 0:
-                nc.vector.tensor_tensor(total[:, 0, :], total[:, 0, :], total[:, 1, :], ALU.add)
-            else:
-                nc.vector.reciprocal(inv[:], total[:, 0, :])
+            w_quantized.append((codes, scales))
 
         for b in range(Q_BLOCKS):
-            w_codes, w_scales = quantize(nc, sb, w_grouped[b], f"w{b}", tag="probs1" if b == 0 else None)
-            res = sb.tile([P, DV], F32, name=f"res{b}")
+            w_codes, w_scales = w_quantized[b]
+            res = sb.tile([P, DV], F32, name=f"res{b}", tag=f"w_grouped{1 - b}", align_bytes=64)
             for h in range(V_BLOCKS):
                 cols = slice(h * P, (h + 1) * P)
                 y = ps.tile([P, P], F32, name=f"y{b}{h}", tag=f"bank{2 * b + h}")

@@ -24,7 +24,8 @@ K_PASS = P * PACK
 PASSES = D // K_PASS
 Q_BLOCKS = NQ // P
 V_BLOCKS = DV // P
-QUADRANTS = 4
+HALF = SLOTS // 2
+SHARE = 256
 
 
 def quantize(nc, sb, grouped, name, tag=None):
@@ -77,12 +78,12 @@ def tile_attend_cap_srt_kernel(tc, qT, k_words, k_scales, vT, vs, offs, out):
 
         vs_slots = sb.tile([P, SLOTS], F32, name="vs_slots")
         nc.vector.tensor_copy(vs_slots[:], vs_pool[:].indirect(offsets[:]))
-        vs_turned = ps.tile([P, PACK, P], F32, name="vs_turned", tag="bank2")
+        vs_turned = ps.tile([P, PACK, P], F32, name="vs_turned", tag="bank4")
         for t in range(PACK):
             nc.tensor.transpose(vs_turned[:, t, :], vs_slots[:, t * P : (t + 1) * P], ident[:])
         vs_cols = sb.tile([P, PACK, 1], F32, name="vs_cols")
         nc.scalar.copy(vs_cols[:], vs_turned[:, :, P - 1 : P])
-        vs_spread = ps.tile([P, SLOTS], F32, name="vs_spread", tag="bank2")
+        vs_spread = ps.tile([P, SLOTS], F32, name="vs_spread", tag="bank4")
         for t in range(PACK):
             nc.tensor.transpose(vs_spread[:, t * P : (t + 1) * P], vs_cols[:, t, :].to_broadcast([P, P]), ident[:])
 
@@ -93,7 +94,10 @@ def tile_attend_cap_srt_kernel(tc, qT, k_words, k_scales, vT, vs, offs, out):
             key_words[:].bitcast(U16), key_pairs[:].bitcast(U16).rearrange("p (n h) -> p h n", h=PASSES)
         )
 
-        scores = [ps.tile([P, SLOTS], F32, name=f"scores{b}", tag=f"bank{b}") for b in range(Q_BLOCKS)]
+        scores = [
+            [ps.tile([P, HALF], F32, name=f"scores{b}{a}", tag=f"bank{2 * b + a}") for a in range(2)]
+            for b in range(Q_BLOCKS)
+        ]
         for o in range(PASSES):
             key_scales = sb.tile(
                 [P, SLOTS], U8, name=f"key_scales{o}", tag="q_raw0" if o == 1 else "key_scales0", align_bytes=64
@@ -106,41 +110,52 @@ def tile_attend_cap_srt_kernel(tc, qT, k_words, k_scales, vT, vs, offs, out):
                     q_raw[o][:, :, b * P : (b + 1) * P].rearrange("p t (c i) -> p c t i", i=4),
                 )
                 codes, scales = quantize(nc, sb, grouped, f"q{o}{b}")
-                nc.tensor.matmul_mx(
-                    out=scores[b][:],
-                    lhsT=codes[:].bitcast(FP8X4),
-                    lhsT_scale=scales[:],
-                    rhs=key_words[:, o, :].bitcast(FP4X4),
-                    rhs_scale=key_scales[:],
-                    start=(o == 0),
-                    stop=(o == PASSES - 1),
-                )
+                for a in range(2):
+                    nc.tensor.matmul_mx(
+                        out=scores[b][a][:],
+                        lhsT=codes[:].bitcast(FP8X4),
+                        lhsT_scale=scales[:],
+                        rhs=key_words[:, o, 2 * a * HALF : 2 * (a + 1) * HALF].bitcast(FP4X4),
+                        rhs_scale=key_scales[:, a * HALF : (a + 1) * HALF],
+                        start=(o == 0),
+                        stop=(o == PASSES - 1),
+                    )
 
-        def gather_values(h, tag):
-            g = sb.tile([P, SLOTS], BF16, name=f"v_slots{h}", tag=tag, align_bytes=64)
-            nc.vector.tensor_copy(g[:], v_pool[h][:].indirect(offsets[:]))
-            return g
+        v_first = sb.tile([P, SLOTS], BF16, name="v_first", tag="q_grouped11", align_bytes=64)
+        nc.vector.tensor_copy(v_first[:], v_pool[0][:].indirect(offsets[:]))
+        v_turned = ps.tile([P, V_BLOCKS, 2, P], F32, name="v_turned", tag="bank5")
+        for u in range(2):
+            nc.tensor.transpose(v_turned[:, 0, u, :], v_first[:].bitcast(F32)[:, u::2], ident[:])
 
-        v_slots = [gather_values(0, "q_raw1"), gather_values(1, "q_grouped11")]
-        v_turned = ps.tile([P, V_BLOCKS, 2, P], F32, name="v_turned", tag="bank3")
-        for h in range(V_BLOCKS):
-            pairs = v_slots[h][:].bitcast(F32)
-            for u in range(2):
-                nc.tensor.transpose(v_turned[:, h, u, :], pairs[:, u::2], ident[:])
+        late = sb.tile([P, SHARE // 2 + SLOTS], F32, name="late", align_bytes=64)
+        nc.vector.memset(late[:, 0:1], 0.0)
+        spare = sb.tile([P, SLOTS], F32, name="spare", tag="v_pool0", align_bytes=64)
+        negated = [spare[:], late[:, SHARE // 2 :]]
 
         capped, neg_max = [], []
         for b in range(Q_BLOCKS):
             c = sb.tile([P, 2, P, 2], F32, name=f"capped{b}", tag=f"capped{b}", align_bytes=64)
-            nc.scalar.activation(
-                c[:], scores[b][:].rearrange("q (s u e) -> q u s e", u=2, e=2), ACT.Tanh, scale=1.0 / CAP
+            for a in range(2):
+                nc.scalar.activation(
+                    c[:, :, a * P // 2 : (a + 1) * P // 2, :],
+                    scores[b][a][:].rearrange("q (s u e) -> q u s e", u=2, e=2),
+                    ACT.Tanh,
+                    bias=late[:, 0:1],
+                    scale=1.0 / CAP,
+                )
+            m = sb.tile([P, 1], F32, name=f"neg_max{b}")
+            nc.vector.tensor_scalar(
+                negated[b], c[:].rearrange("q u s e -> q (u s e)"), -CAP, None, op0=ALU.mult, op1=ALU.min, accum_out=m[:]
             )
             capped.append(c)
-            m = sb.tile([P, 1], F32, name=f"neg_max{b}")
-            negated = sb.tile([P, SLOTS], F32, name=f"negated{b}", tag=f"v_pool{1 - b}", align_bytes=64)
-            nc.vector.tensor_scalar(
-                negated[:], c[:].rearrange("q u s e -> q (u s e)"), -CAP, None, op0=ALU.mult, op1=ALU.min, accum_out=m[:]
-            )
             neg_max.append(m)
+
+        v_late = late[:, 0:HALF].bitcast(BF16)
+        nc.scalar.activation(v_late[:, 0:SHARE], v_pool[1][:].indirect(offsets[:, 0 : SHARE // 16]), ACT.Copy)
+        nc.vector.tensor_copy(v_late[:, SHARE:], v_pool[1][:].indirect(offsets[:, SHARE // 16 :]))
+        for u in range(2):
+            nc.tensor.transpose(v_turned[:, 1, u, :], late[:, u:HALF:2], ident[:])
+
         total = sb.tile([P, 2, Q_BLOCKS], F32, name="total")
         vs_halves = vs_spread[:].rearrange("q (s u e) -> q u s e", u=2, e=2)
         w_turned = []
@@ -167,7 +182,7 @@ def tile_attend_cap_srt_kernel(tc, qT, k_words, k_scales, vT, vs, offs, out):
         for b in range(Q_BLOCKS):
             w_grouped.append(sb.tile([P, P, 2], F32, name=f"w_grouped{b}", tag=f"w_grouped{b}", align_bytes=64))
         nc.vector.tensor_copy(w_grouped[0][:], w_turned[0][:].rearrange("s u q -> s q u"))
-        v_grouped = sb.tile([P, V_BLOCKS, P, 2], F32, name="v_grouped", tag="capped0", align_bytes=64)
+        v_grouped = sb.tile([P, V_BLOCKS, P, 2], F32, name="v_grouped", tag="capped1", align_bytes=64)
         nc.scalar.copy(v_grouped[:], v_turned[:].rearrange("s h u e -> s h e u"))
         v_codes = sb.tile([P, DV], U32, name="v_codes", align_bytes=64)
         v_scales = sb.tile([P, DV], U8, name="v_scales", align_bytes=64)

@@ -25,7 +25,6 @@ PASSES = D // K_PASS
 Q_BLOCKS = NQ // P
 V_BLOCKS = DV // P
 HALF = SLOTS // 2
-SHARE = 256
 
 
 def quantize(nc, sb, grouped, name, tag=None):
@@ -121,16 +120,17 @@ def tile_attend_cap_srt_kernel(tc, qT, k_words, k_scales, vT, vs, offs, out):
                         stop=(o == PASSES - 1),
                     )
 
-        v_first = sb.tile([P, SLOTS], BF16, name="v_first", tag="q_grouped11", align_bytes=64)
-        nc.vector.tensor_copy(v_first[:], v_pool[0][:].indirect(offsets[:]))
-        v_turned = ps.tile([P, V_BLOCKS, 2, P], F32, name="v_turned", tag="bank5")
-        for u in range(2):
-            nc.tensor.transpose(v_turned[:, 0, u, :], v_first[:].bitcast(F32)[:, u::2], ident[:])
+        def gather_values(h, tag):
+            g = sb.tile([P, SLOTS], BF16, name=f"v_slots{h}", tag=tag, align_bytes=64)
+            nc.vector.tensor_copy(g[:], v_pool[h][:].indirect(offsets[:]))
+            return g
 
-        late = sb.tile([P, SHARE // 2 + SLOTS], F32, name="late", align_bytes=64)
-        nc.vector.memset(late[:, 0:1], 0.0)
-        spare = sb.tile([P, SLOTS], F32, name="spare", tag="v_pool0", align_bytes=64)
-        negated = [spare[:], late[:, SHARE // 2 :]]
+        v_slots = [gather_values(0, "q_raw1"), gather_values(1, "q_grouped11")]
+        v_turned = ps.tile([P, V_BLOCKS, 2, P], F32, name="v_turned", tag="bank5")
+        for h in range(V_BLOCKS):
+            pairs = v_slots[h][:].bitcast(F32)
+            for u in range(2):
+                nc.tensor.transpose(v_turned[:, h, u, :], pairs[:, u::2], ident[:])
 
         capped, neg_max = [], []
         for b in range(Q_BLOCKS):
@@ -140,21 +140,15 @@ def tile_attend_cap_srt_kernel(tc, qT, k_words, k_scales, vT, vs, offs, out):
                     c[:, :, a * P // 2 : (a + 1) * P // 2, :],
                     scores[b][a][:].rearrange("q (s u e) -> q u s e", u=2, e=2),
                     ACT.Tanh,
-                    bias=late[:, 0:1],
                     scale=1.0 / CAP,
                 )
             m = sb.tile([P, 1], F32, name=f"neg_max{b}")
+            negated = sb.tile([P, SLOTS], F32, name=f"negated{b}", tag=f"v_pool{1 - b}", align_bytes=64)
             nc.vector.tensor_scalar(
-                negated[b], c[:].rearrange("q u s e -> q (u s e)"), -CAP, None, op0=ALU.mult, op1=ALU.min, accum_out=m[:]
+                negated[:], c[:].rearrange("q u s e -> q (u s e)"), -CAP, None, op0=ALU.mult, op1=ALU.min, accum_out=m[:]
             )
             capped.append(c)
             neg_max.append(m)
-
-        v_late = late[:, 0:HALF].bitcast(BF16)
-        nc.scalar.activation(v_late[:, 0:SHARE], v_pool[1][:].indirect(offsets[:, 0 : SHARE // 16]), ACT.Copy)
-        nc.vector.tensor_copy(v_late[:, SHARE:], v_pool[1][:].indirect(offsets[:, SHARE // 16 :]))
-        for u in range(2):
-            nc.tensor.transpose(v_turned[:, 1, u, :], late[:, u:HALF:2], ident[:])
 
         total = sb.tile([P, 2, Q_BLOCKS], F32, name="total")
         vs_halves = vs_spread[:].rearrange("q (s u e) -> q u s e", u=2, e=2)
@@ -182,7 +176,7 @@ def tile_attend_cap_srt_kernel(tc, qT, k_words, k_scales, vT, vs, offs, out):
         for b in range(Q_BLOCKS):
             w_grouped.append(sb.tile([P, P, 2], F32, name=f"w_grouped{b}", tag=f"w_grouped{b}", align_bytes=64))
         nc.vector.tensor_copy(w_grouped[0][:], w_turned[0][:].rearrange("s u q -> s q u"))
-        v_grouped = sb.tile([P, V_BLOCKS, P, 2], F32, name="v_grouped", tag="capped1", align_bytes=64)
+        v_grouped = sb.tile([P, V_BLOCKS, P, 2], F32, name="v_grouped", tag="capped0", align_bytes=64)
         nc.scalar.copy(v_grouped[:], v_turned[:].rearrange("s h u e -> s h e u"))
         v_codes = sb.tile([P, DV], U32, name="v_codes", align_bytes=64)
         v_scales = sb.tile([P, DV], U8, name="v_scales", align_bytes=64)

@@ -122,7 +122,10 @@ def tile_attend_cap_srt_kernel(tc, qT, k_words, k_scales, vT, vs, offs, out):
 
         def gather_values(h, tag):
             g = sb.tile([P, SLOTS], BF16, name=f"v_slots{h}", tag=tag, align_bytes=64)
-            nc.vector.tensor_copy(g[:], v_pool[h][:].indirect(offsets[:]))
+            if h == 0:
+                nc.scalar.activation(g[:], v_pool[h][:].indirect(offsets[:]), ACT.Copy)
+            else:
+                nc.vector.tensor_copy(g[:], v_pool[h][:].indirect(offsets[:]))
             return g
 
         v_slots = [gather_values(0, "q_raw1"), gather_values(1, "q_grouped11")]

@@ -25,16 +25,8 @@ PASSES = D // K_PASS
 Q_BLOCKS = NQ // P
 V_BLOCKS = DV // P
 HALF = SLOTS // 2
-
-
-def quantize(nc, sb, grouped, name, tag=None):
-    width = grouped.shape[1]
-    codes = sb.tile([P, width], U32, name=name + "_codes", tag=tag or name + "_codes", align_bytes=64)
-    scales = sb.tile([P, width], U8, name=name + "_scales", align_bytes=64)
-    nc.vector.quantize_mx(
-        out=codes[:].bitcast(FP8X4), scales=scales[:], in_=grouped[:].rearrange("p c t -> p (c t)")
-    )
-    return codes, scales
+VECTOR_SHARE = 224
+LATE_START = 320
 
 
 def tile_attend_cap_srt_kernel(tc, qT, k_words, k_scales, vT, vs, offs, out):
@@ -97,43 +89,43 @@ def tile_attend_cap_srt_kernel(tc, qT, k_words, k_scales, vT, vs, offs, out):
             [ps.tile([P, HALF], F32, name=f"scores{b}{a}", tag=f"bank{2 * b + a}") for a in range(2)]
             for b in range(Q_BLOCKS)
         ]
+        shared = sb.tile([P, LATE_START + SLOTS], BF16, name="shared", align_bytes=64)
+        late_values = shared[:, LATE_START : LATE_START + SLOTS]
+        zero_bias = late_values[:, SLOTS - 1 : SLOTS]
+        nc.vector.memset(zero_bias, 0.0)
         for o in range(PASSES):
             key_scales = sb.tile(
                 [P, SLOTS], U8, name=f"key_scales{o}", tag="q_raw0" if o == 1 else "key_scales0", align_bytes=64
             )
             nc.vector.tensor_copy(key_scales[:], scale_pool[:, o, :].bitcast(U8).indirect(offsets[:]))
             for b in range(Q_BLOCKS):
-                grouped = sb.tile([P, P, PACK], BF16, name=f"q_grouped{o}{b}", tag=f"q_grouped{o}{b}", align_bytes=64)
+                if (o, b) == (PASSES - 1, Q_BLOCKS - 1):
+                    grouped = shared[:, 0:K_PASS]
+                else:
+                    grouped = sb.tile([P, K_PASS], BF16, name=f"q_grouped{o}{b}", align_bytes=64)[:]
                 nc.scalar.copy(
-                    grouped[:].rearrange("p (c i) t -> p c t i", i=4),
+                    grouped.rearrange("p (c i t) -> p c t i", i=4, t=PACK),
                     q_raw[o][:, :, b * P : (b + 1) * P].rearrange("p t (c i) -> p c t i", i=4),
                 )
-                codes, scales = quantize(nc, sb, grouped, f"q{o}{b}")
+                codes = sb.tile([P, P], U32, name=f"q_codes{o}{b}", align_bytes=64)[:]
+                scales = sb.tile([P, P], U8, name=f"q_scales{o}{b}", align_bytes=64)[:]
+                nc.vector.quantize_mx(out=codes.bitcast(FP8X4), scales=scales, in_=grouped)
                 for a in range(2):
                     nc.tensor.matmul_mx(
                         out=scores[b][a][:],
-                        lhsT=codes[:].bitcast(FP8X4),
-                        lhsT_scale=scales[:],
+                        lhsT=codes.bitcast(FP8X4),
+                        lhsT_scale=scales,
                         rhs=key_words[:, o, 2 * a * HALF : 2 * (a + 1) * HALF].bitcast(FP4X4),
                         rhs_scale=key_scales[:, a * HALF : (a + 1) * HALF],
                         start=(o == 0),
                         stop=(o == PASSES - 1),
                     )
 
-        def gather_values(h, tag):
-            g = sb.tile([P, SLOTS], BF16, name=f"v_slots{h}", tag=tag, align_bytes=64)
-            if h == 0:
-                nc.scalar.activation(g[:], v_pool[h][:].indirect(offsets[:]), ACT.Copy)
-            else:
-                nc.vector.tensor_copy(g[:], v_pool[h][:].indirect(offsets[:]))
-            return g
-
-        v_slots = [gather_values(0, "q_raw1"), gather_values(1, "q_grouped11")]
-        v_turned = ps.tile([P, V_BLOCKS, 2, P], F32, name="v_turned", tag="bank5")
-        for h in range(V_BLOCKS):
-            pairs = v_slots[h][:].bitcast(F32)
-            for u in range(2):
-                nc.tensor.transpose(v_turned[:, h, u, :], pairs[:, u::2], ident[:])
+        early_values = sb.tile([P, SLOTS], BF16, name="early_values", tag="q_raw1", align_bytes=64)
+        nc.vector.tensor_copy(early_values[:], v_pool[0][:].indirect(offsets[:]))
+        nc.vector.tensor_copy(
+            late_values[:, 0:VECTOR_SHARE], v_pool[1][:].indirect(offsets[:, 0 : VECTOR_SHARE // 16])
+        )
 
         capped, neg_max = [], []
         for b in range(Q_BLOCKS):
@@ -143,15 +135,27 @@ def tile_attend_cap_srt_kernel(tc, qT, k_words, k_scales, vT, vs, offs, out):
                     c[:, :, a * P // 2 : (a + 1) * P // 2, :],
                     scores[b][a][:].rearrange("q (s u e) -> q u s e", u=2, e=2),
                     ACT.Tanh,
+                    bias=zero_bias if (b, a) == (Q_BLOCKS - 1, 0) else 0.0,
                     scale=1.0 / CAP,
                 )
             m = sb.tile([P, 1], F32, name=f"neg_max{b}")
-            negated = sb.tile([P, SLOTS], F32, name=f"negated{b}", tag=f"v_pool{1 - b}", align_bytes=64)
+            negated = sb.tile([P, SLOTS], F32, name=f"negated{b}", align_bytes=64)
             nc.vector.tensor_scalar(
                 negated[:], c[:].rearrange("q u s e -> q (u s e)"), -CAP, None, op0=ALU.mult, op1=ALU.min, accum_out=m[:]
             )
             capped.append(c)
             neg_max.append(m)
+
+        nc.scalar.activation(
+            late_values[:, VECTOR_SHARE:SLOTS],
+            v_pool[1][:].indirect(offsets[:, VECTOR_SHARE // 16 : SLOTS // 16]),
+            ACT.Copy,
+        )
+        v_turned = ps.tile([P, V_BLOCKS, 2, P], F32, name="v_turned", tag="bank5")
+        for h, values in enumerate((early_values[:], late_values)):
+            pairs = values.bitcast(F32)
+            for u in range(2):
+                nc.tensor.transpose(v_turned[:, h, u, :], pairs[:, u::2], ident[:])
 
         total = sb.tile([P, 2, Q_BLOCKS], F32, name="total")
         vs_halves = vs_spread[:].rearrange("q (s u e) -> q u s e", u=2, e=2)

@@ -25,8 +25,16 @@ PASSES = D // K_PASS
 Q_BLOCKS = NQ // P
 V_BLOCKS = DV // P
 HALF = SLOTS // 2
-VECTOR_SHARE = 224
-LATE_START = 320
+
+
+def quantize(nc, sb, grouped, name):
+    width = grouped.shape[1]
+    codes = sb.tile([P, width], U32, name=name + "_codes", align_bytes=64)
+    scales = sb.tile([P, width], U8, name=name + "_scales", align_bytes=64)
+    nc.vector.quantize_mx(
+        out=codes[:].bitcast(FP8X4), scales=scales[:], in_=grouped[:].rearrange("p c t -> p (c t)")
+    )
+    return codes, scales
 
 
 def tile_attend_cap_srt_kernel(tc, qT, k_words, k_scales, vT, vs, offs, out):
@@ -89,43 +97,39 @@ def tile_attend_cap_srt_kernel(tc, qT, k_words, k_scales, vT, vs, offs, out):
             [ps.tile([P, HALF], F32, name=f"scores{b}{a}", tag=f"bank{2 * b + a}") for a in range(2)]
             for b in range(Q_BLOCKS)
         ]
-        shared = sb.tile([P, LATE_START + SLOTS], BF16, name="shared", align_bytes=64)
-        late_values = shared[:, LATE_START : LATE_START + SLOTS]
-        zero_bias = late_values[:, SLOTS - 1 : SLOTS]
-        nc.vector.memset(zero_bias, 0.0)
         for o in range(PASSES):
             key_scales = sb.tile(
                 [P, SLOTS], U8, name=f"key_scales{o}", tag="q_raw0" if o == 1 else "key_scales0", align_bytes=64
             )
             nc.vector.tensor_copy(key_scales[:], scale_pool[:, o, :].bitcast(U8).indirect(offsets[:]))
             for b in range(Q_BLOCKS):
-                if (o, b) == (PASSES - 1, Q_BLOCKS - 1):
-                    grouped = shared[:, 0:K_PASS]
-                else:
-                    grouped = sb.tile([P, K_PASS], BF16, name=f"q_grouped{o}{b}", align_bytes=64)[:]
+                grouped = sb.tile([P, P, PACK], BF16, name=f"q_grouped{o}{b}", tag=f"q_grouped{o}{b}", align_bytes=64)
                 nc.scalar.copy(
-                    grouped.rearrange("p (c i t) -> p c t i", i=4, t=PACK),
+                    grouped[:].rearrange("p (c i) t -> p c t i", i=4),
                     q_raw[o][:, :, b * P : (b + 1) * P].rearrange("p t (c i) -> p c t i", i=4),
                 )
-                codes = sb.tile([P, P], U32, name=f"q_codes{o}{b}", align_bytes=64)[:]
-                scales = sb.tile([P, P], U8, name=f"q_scales{o}{b}", align_bytes=64)[:]
-                nc.vector.quantize_mx(out=codes.bitcast(FP8X4), scales=scales, in_=grouped)
+                codes, scales = quantize(nc, sb, grouped, f"q{o}{b}")
                 for a in range(2):
                     nc.tensor.matmul_mx(
                         out=scores[b][a][:],
-                        lhsT=codes.bitcast(FP8X4),
-                        lhsT_scale=scales,
+                        lhsT=codes[:].bitcast(FP8X4),
+                        lhsT_scale=scales[:],
                         rhs=key_words[:, o, 2 * a * HALF : 2 * (a + 1) * HALF].bitcast(FP4X4),
                         rhs_scale=key_scales[:, a * HALF : (a + 1) * HALF],
                         start=(o == 0),
                         stop=(o == PASSES - 1),
                     )
 
-        early_values = sb.tile([P, SLOTS], BF16, name="early_values", tag="q_raw1", align_bytes=64)
-        nc.vector.tensor_copy(early_values[:], v_pool[0][:].indirect(offsets[:]))
-        nc.vector.tensor_copy(
-            late_values[:, 0:VECTOR_SHARE], v_pool[1][:].indirect(offsets[:, 0 : VECTOR_SHARE // 16])
-        )
+        v_slots = []
+        for h, tag in enumerate(("q_raw1", "q_grouped11")):
+            g = sb.tile([P, SLOTS], BF16, name=f"v_slots{h}", tag=tag, align_bytes=64)
+            nc.vector.tensor_copy(g[:], v_pool[h][:].indirect(offsets[:]))
+            v_slots.append(g)
+        v_turned = ps.tile([P, V_BLOCKS, 2, P], F32, name="v_turned", tag="bank5")
+        for h in range(V_BLOCKS):
+            pairs = v_slots[h][:].bitcast(F32)
+            for u in range(2):
+                nc.tensor.transpose(v_turned[:, h, u, :], pairs[:, u::2], ident[:])
 
         capped, neg_max = [], []
         for b in range(Q_BLOCKS):
@@ -135,56 +139,43 @@ def tile_attend_cap_srt_kernel(tc, qT, k_words, k_scales, vT, vs, offs, out):
                     c[:, :, a * P // 2 : (a + 1) * P // 2, :],
                     scores[b][a][:].rearrange("q (s u e) -> q u s e", u=2, e=2),
                     ACT.Tanh,
-                    bias=zero_bias if (b, a) == (Q_BLOCKS - 1, 0) else 0.0,
                     scale=1.0 / CAP,
                 )
             m = sb.tile([P, 1], F32, name=f"neg_max{b}")
-            negated = sb.tile([P, SLOTS], F32, name=f"negated{b}", align_bytes=64)
+            negated = sb.tile([P, SLOTS], F32, name=f"negated{b}", tag=f"negated{b}", align_bytes=64)
             nc.vector.tensor_scalar(
                 negated[:], c[:].rearrange("q u s e -> q (u s e)"), -CAP, None, op0=ALU.mult, op1=ALU.min, accum_out=m[:]
             )
             capped.append(c)
             neg_max.append(m)
 
-        nc.scalar.activation(
-            late_values[:, VECTOR_SHARE:SLOTS],
-            v_pool[1][:].indirect(offsets[:, VECTOR_SHARE // 16 : SLOTS // 16]),
-            ACT.Copy,
-        )
-        v_turned = ps.tile([P, V_BLOCKS, 2, P], F32, name="v_turned", tag="bank5")
-        for h, values in enumerate((early_values[:], late_values)):
-            pairs = values.bitcast(F32)
-            for u in range(2):
-                nc.tensor.transpose(v_turned[:, h, u, :], pairs[:, u::2], ident[:])
-
         total = sb.tile([P, 2, Q_BLOCKS], F32, name="total")
+        shift = sb.tile([P, Q_BLOCKS], F32, name="shift")
         vs_halves = vs_spread[:].rearrange("q (s u e) -> q u s e", u=2, e=2)
         w_turned = []
         for b in range(Q_BLOCKS):
-            pr = sb.tile([P, 2, P, 2], F32, name=f"probs{b}", align_bytes=64)
             w = sb.tile([P, 2, P, 2], BF16, name=f"w{b}", align_bytes=64)
             turned = ps.tile([P, 2, P], F32, name=f"w_turned{b}")
+            nc.scalar.activation(shift[:, b : b + 1], neg_max[b][:], ACT.Exp)
             for u in range(2):
-                nc.scalar.activation(
-                    pr[:, u],
-                    capped[b][:, u],
-                    ACT.Exp,
-                    bias=neg_max[b][:],
-                    scale=CAP,
-                    accum_out=total[:, u, b : b + 1],
+                grown = sb.tile(
+                    [P, P, 2], F32, name=f"grown{b}{u}", tag=f"negated{u}" if b == 1 else f"grown{u}", align_bytes=64
                 )
-                nc.vector.tensor_tensor(w[:, u], pr[:, u], vs_halves[:, u], ALU.mult)
+                nc.scalar.activation(grown[:], capped[b][:, u], ACT.Exp, scale=CAP, accum_out=total[:, u, b : b + 1])
+                nc.vector.scalar_tensor_tensor(
+                    w[:, u], grown[:], shift[:, b : b + 1], vs_halves[:, u], op0=ALU.mult, op1=ALU.mult
+                )
                 nc.tensor.transpose(turned[:, u, :], w[:, u].rearrange("q s e -> q (s e)").bitcast(F32), ident[:])
             w_turned.append(turned)
 
         inv = sb.tile([P, Q_BLOCKS], F32, name="inv")
         nc.vector.tensor_tensor(total[:, 0, :], total[:, 0, :], total[:, 1, :], ALU.add)
+        v_grouped = sb.tile([P, V_BLOCKS, P, 2], F32, name="v_grouped", tag="capped1", align_bytes=64)
+        nc.scalar.copy(v_grouped[:], v_turned[:].rearrange("s h u e -> s h e u"))
         w_grouped = []
         for b in range(Q_BLOCKS):
             w_grouped.append(sb.tile([P, P, 2], F32, name=f"w_grouped{b}", tag=f"w_grouped{b}", align_bytes=64))
-        nc.vector.tensor_copy(w_grouped[0][:], w_turned[0][:].rearrange("s u q -> s q u"))
-        v_grouped = sb.tile([P, V_BLOCKS, P, 2], F32, name="v_grouped", tag="capped0", align_bytes=64)
-        nc.scalar.copy(v_grouped[:], v_turned[:].rearrange("s h u e -> s h e u"))
+        nc.vector.tensor_tensor(total[:, 1, :], total[:, 0, :], shift[:], ALU.mult)
         v_codes = sb.tile([P, DV], U32, name="v_codes", align_bytes=64)
         v_scales = sb.tile([P, DV], U8, name="v_scales", align_bytes=64)
         nc.vector.quantize_mx(
@@ -192,13 +183,12 @@ def tile_attend_cap_srt_kernel(tc, qT, k_words, k_scales, vT, vs, offs, out):
             scales=v_scales[:],
             in_=v_grouped[:].rearrange("s h e u -> s (h e u)").bitcast(BF16),
         )
-        nc.vector.reciprocal(inv[:], total[:, 0, :])
+        nc.vector.reciprocal(inv[:], total[:, 1, :])
 
         w_quantized = []
         for b in range(Q_BLOCKS):
             grouped = w_grouped[b]
-            if b == 1:
-                nc.scalar.copy(grouped[:], w_turned[b][:].rearrange("s u q -> s q u"))
+            nc.scalar.copy(grouped[:], w_turned[b][:].rearrange("s u q -> s q u"))
             codes = sb.tile([P, P], U32, name=f"w_codes{b}", align_bytes=64)
             scales = sb.tile([P, P], U8, name=f"w_scales{b}", align_bytes=64)
             nc.vector.quantize_mx(

@@ -80,11 +80,13 @@ def tile_attend_cap_srt_kernel(tc, qT, k_words, k_scales, vT, vs, offs, out):
         vs_turned = ps.tile([P, PACK, P], F32, name="vs_turned", tag="bank4")
         for t in range(PACK):
             nc.tensor.transpose(vs_turned[:, t, :], vs_slots[:, t * P : (t + 1) * P], ident[:])
-        vs_cols = sb.tile([P, PACK, 1], F32, name="vs_cols")
-        nc.scalar.copy(vs_cols[:], vs_turned[:, :, P - 1 : P])
+        zero_bias = sb.tile([P, 1], F32, name="zero_bias", tag="zero_bias", align_bytes=64)
+        nc.scalar.copy(zero_bias[:], vs_turned[:, 0, 0:1])
+        vs_cols = sb.tile([P, PACK, 2], F32, name="vs_cols")
+        nc.scalar.copy(vs_cols[:], vs_turned[:, :, P - 2 : P])
         vs_spread = ps.tile([P, SLOTS], F32, name="vs_spread", tag="bank4")
         for t in range(PACK):
-            nc.tensor.transpose(vs_spread[:, t * P : (t + 1) * P], vs_cols[:, t, :].to_broadcast([P, P]), ident[:])
+            nc.tensor.transpose(vs_spread[:, t * P : (t + 1) * P], vs_cols[:, t, 1:2].to_broadcast([P, P]), ident[:])
 
         key_pairs = sb.tile([P, SLOTS], U32, name="key_pairs")
         nc.vector.tensor_copy(key_pairs[:], key_pool[:].bitcast(U32).indirect(offsets[:]))
@@ -97,25 +99,31 @@ def tile_attend_cap_srt_kernel(tc, qT, k_words, k_scales, vT, vs, offs, out):
             [ps.tile([P, HALF], F32, name=f"scores{b}{a}", tag=f"bank{2 * b + a}") for a in range(2)]
             for b in range(Q_BLOCKS)
         ]
+        first_scales = sb.tile([P, SLOTS], U8, name="first_scales", align_bytes=64)
+        nc.vector.tensor_copy(first_scales[:], scale_pool[:, 0, :].bitcast(U8).indirect(offsets[:]))
+        key_scales = [[first_scales[:, 0:HALF], first_scales[:, HALF:SLOTS]], []]
         for o in range(PASSES):
-            key_scales = sb.tile(
-                [P, SLOTS], U8, name=f"key_scales{o}", tag="q_raw0" if o == 1 else "key_scales0", align_bytes=64
-            )
-            nc.vector.tensor_copy(key_scales[:], scale_pool[:, o, :].bitcast(U8).indirect(offsets[:]))
             for b in range(Q_BLOCKS):
                 grouped = sb.tile([P, P, PACK], BF16, name=f"q_grouped{o}{b}", tag=f"q_grouped{o}{b}", align_bytes=64)
-                nc.scalar.copy(
-                    grouped[:].rearrange("p (c i) t -> p c t i", i=4),
-                    q_raw[o][:, :, b * P : (b + 1) * P].rearrange("p t (c i) -> p c t i", i=4),
-                )
+                rounded = grouped[:].rearrange("p (c i) t -> p c t i", i=4)
+                raw = q_raw[o][:, :, b * P : (b + 1) * P].rearrange("p t (c i) -> p c t i", i=4)
+                bias = zero_bias[:] if (o, b) == (0, 0) else vs_cols[:, 0, 0:1]
+                nc.scalar.activation(rounded, raw, ACT.Identity, bias=bias)
                 codes, scales = quantize(nc, sb, grouped, f"q{o}{b}")
+                if o == 0:
+                    half = sb.tile(
+                        [P, HALF], U8, name=f"second_scales{b}", tag=("zero_bias", "q_raw0")[b], align_bytes=64
+                    )
+                    half_list = offsets[:, b * HALF // 16 : (b + 1) * HALF // 16]
+                    nc.vector.tensor_copy(half[:], scale_pool[:, 1, :].bitcast(U8).indirect(half_list))
+                    key_scales[1].append(half[:])
                 for a in range(2):
                     nc.tensor.matmul_mx(
                         out=scores[b][a][:],
                         lhsT=codes[:].bitcast(FP8X4),
                         lhsT_scale=scales[:],
                         rhs=key_words[:, o, 2 * a * HALF : 2 * (a + 1) * HALF].bitcast(FP4X4),
-                        rhs_scale=key_scales[:, a * HALF : (a + 1) * HALF],
+                        rhs_scale=key_scales[o][a],
                         start=(o == 0),
                         stop=(o == PASSES - 1),
                     )
@@ -142,9 +150,8 @@ def tile_attend_cap_srt_kernel(tc, qT, k_words, k_scales, vT, vs, offs, out):
                     scale=1.0 / CAP,
                 )
             m = sb.tile([P, 1], F32, name=f"neg_max{b}")
-            negated = sb.tile([P, SLOTS], F32, name=f"negated{b}", tag=f"negated{b}", align_bytes=64)
-            nc.vector.tensor_scalar(
-                negated[:], c[:].rearrange("q u s e -> q (u s e)"), -CAP, None, op0=ALU.mult, op1=ALU.min, accum_out=m[:]
+            nc.vector.tensor_reduce(
+                m[:], c[:].rearrange("q u s e -> q (u s e)"), mybir.AxisListType.X, ALU.max, negate=True
             )
             capped.append(c)
             neg_max.append(m)
@@ -156,21 +163,22 @@ def tile_attend_cap_srt_kernel(tc, qT, k_words, k_scales, vT, vs, offs, out):
         for b in range(Q_BLOCKS):
             w = sb.tile([P, 2, P, 2], BF16, name=f"w{b}", align_bytes=64)
             turned = ps.tile([P, 2, P], F32, name=f"w_turned{b}")
-            nc.scalar.activation(shift[:, b : b + 1], neg_max[b][:], ACT.Exp)
+            nc.scalar.activation(shift[:, b : b + 1], neg_max[b][:], ACT.Exp, scale=CAP)
             for u in range(2):
-                grown = sb.tile(
-                    [P, P, 2], F32, name=f"grown{b}{u}", tag=f"negated{u}" if b == 1 else f"grown{u}", align_bytes=64
-                )
-                nc.scalar.activation(grown[:], capped[b][:, u], ACT.Exp, scale=CAP, accum_out=total[:, u, b : b + 1])
+                if b == 0:
+                    grown = sb.tile([P, P, 2], F32, name=f"grown{u}", tag=f"grown{u}", align_bytes=64)[:]
+                else:
+                    grown = capped[u][:, 0]
+                nc.scalar.activation(grown, capped[b][:, u], ACT.Exp, scale=CAP, accum_out=total[:, u, b : b + 1])
                 nc.vector.scalar_tensor_tensor(
-                    w[:, u], grown[:], shift[:, b : b + 1], vs_halves[:, u], op0=ALU.mult, op1=ALU.mult
+                    w[:, u], grown, shift[:, b : b + 1], vs_halves[:, u], op0=ALU.mult, op1=ALU.mult
                 )
                 nc.tensor.transpose(turned[:, u, :], w[:, u].rearrange("q s e -> q (s e)").bitcast(F32), ident[:])
             w_turned.append(turned)
 
         inv = sb.tile([P, Q_BLOCKS], F32, name="inv")
         nc.vector.tensor_tensor(total[:, 0, :], total[:, 0, :], total[:, 1, :], ALU.add)
-        v_grouped = sb.tile([P, V_BLOCKS, P, 2], F32, name="v_grouped", tag="capped1", align_bytes=64)
+        v_grouped = sb.tile([P, V_BLOCKS, P, 2], F32, name="v_grouped", tag="grown1", align_bytes=64)
         nc.scalar.copy(v_grouped[:], v_turned[:].rearrange("s h u e -> s h e u"))
         w_grouped = []
         for b in range(Q_BLOCKS):

@@ -25,6 +25,7 @@ PASSES = D // K_PASS
 Q_BLOCKS = NQ // P
 V_BLOCKS = DV // P
 HALF = SLOTS // 2
+SCALAR_SHARE = 192
 
 
 def quantize(nc, sb, grouped, name):
@@ -131,7 +132,10 @@ def tile_attend_cap_srt_kernel(tc, qT, k_words, k_scales, vT, vs, offs, out):
         v_slots = []
         for h, tag in enumerate(("q_raw1", "q_grouped11")):
             g = sb.tile([P, SLOTS], BF16, name=f"v_slots{h}", tag=tag, align_bytes=64)
-            nc.vector.tensor_copy(g[:], v_pool[h][:].indirect(offsets[:]))
+            first = SCALAR_SHARE if h == 0 else 0
+            if first:
+                nc.scalar.activation(g[:, 0:first], v_pool[h][:].indirect(offsets[:, 0 : first // 16]), ACT.Copy)
+            nc.vector.tensor_copy(g[:, first:SLOTS], v_pool[h][:].indirect(offsets[:, first // 16 : SLOTS // 16]))
             v_slots.append(g)
         v_turned = ps.tile([P, V_BLOCKS, 2, P], F32, name="v_turned", tag="bank5")
         for h in range(V_BLOCKS):

@@ -199,13 +199,18 @@ def tile_attend_cap_srt_kernel(tc, qT, k_words, k_scales, vT, vs, offs, out):
 
         w_quantized = []
         for b in range(Q_BLOCKS):
-            grouped = w_grouped[b]
-            nc.scalar.copy(grouped[:], w_turned[b][:].rearrange("s u q -> s q u"))
             codes = sb.tile([P, P], U32, name=f"w_codes{b}", align_bytes=64)
             scales = sb.tile([P, P], U8, name=f"w_scales{b}", align_bytes=64)
-            nc.vector.quantize_mx(
-                out=codes[:].bitcast(FP8X4), scales=scales[:], in_=grouped[:].rearrange("s q u -> s (q u)").bitcast(BF16)
-            )
+            pieces = b + 1
+            for piece in range(pieces):
+                rows = slice(piece * P // pieces, (piece + 1) * P // pieces)
+                grouped = w_grouped[b][:, rows, :]
+                nc.scalar.copy(grouped, w_turned[b][:, :, rows].rearrange("s u q -> s q u"))
+                nc.vector.quantize_mx(
+                    out=codes[:, rows].bitcast(FP8X4),
+                    scales=scales[:, rows],
+                    in_=grouped.rearrange("s q u -> s (q u)").bitcast(BF16),
+                )
             w_quantized.append((codes, scales))
 
         for b in range(Q_BLOCKS):

@@ -25,6 +25,7 @@ PASSES = D // K_PASS
 Q_BLOCKS = NQ // P
 V_BLOCKS = DV // P
 HALF = SLOTS // 2
+ROUNDED_BYTES = 2 * K_PASS
 SCALAR_SHARE = 192
 
 
@@ -42,6 +43,7 @@ def tile_attend_cap_srt_kernel(tc, qT, k_words, k_scales, vT, vs, offs, out):
     nc = tc.nc
     with ExitStack() as ctx:
         sb = ctx.enter_context(tc.tile_pool(name="sb", bufs=1))
+        reused = ctx.enter_context(tc.tile_pool(name="reused", bufs=1))
         ps = ctx.enter_context(tc.psum_pool(name="ps", bufs=1))
 
         vs_pool = sb.tile([P, TOKENS], F32, name="vs_pool")
@@ -76,18 +78,16 @@ def tile_attend_cap_srt_kernel(tc, qT, k_words, k_scales, vT, vs, offs, out):
             nc.sync.dma_start(t[:], vT[h * P : (h + 1) * P, :])
             v_pool.append(t)
 
-        vs_slots = sb.tile([P, SLOTS], F32, name="vs_slots")
+        vs_slots = reused.tile([P, SLOTS], F32, name="vs_slots", align_bytes=64, offset=ROUNDED_BYTES - 64)
         nc.vector.tensor_copy(vs_slots[:], vs_pool[:].indirect(offsets[:]))
         vs_turned = ps.tile([P, PACK, P], F32, name="vs_turned", tag="bank4")
         for t in range(PACK):
             nc.tensor.transpose(vs_turned[:, t, :], vs_slots[:, t * P : (t + 1) * P], ident[:])
-        zero_bias = sb.tile([P, 1], F32, name="zero_bias", tag="zero_bias", align_bytes=64)
-        nc.scalar.copy(zero_bias[:], vs_turned[:, 0, 0:1])
-        vs_cols = sb.tile([P, PACK, 2], F32, name="vs_cols")
-        nc.scalar.copy(vs_cols[:], vs_turned[:, :, P - 2 : P])
+        vs_cols = sb.tile([P, PACK, 1], F32, name="vs_cols", tag="vs_cols", align_bytes=64)
+        nc.scalar.copy(vs_cols[:], vs_turned[:, :, P - 1 : P])
         vs_spread = ps.tile([P, SLOTS], F32, name="vs_spread", tag="bank4")
         for t in range(PACK):
-            nc.tensor.transpose(vs_spread[:, t * P : (t + 1) * P], vs_cols[:, t, 1:2].to_broadcast([P, P]), ident[:])
+            nc.tensor.transpose(vs_spread[:, t * P : (t + 1) * P], vs_cols[:, t, :].to_broadcast([P, P]), ident[:])
 
         key_pairs = sb.tile([P, SLOTS], U32, name="key_pairs")
         nc.vector.tensor_copy(key_pairs[:], key_pool[:].bitcast(U32).indirect(offsets[:]))
@@ -105,15 +105,17 @@ def tile_attend_cap_srt_kernel(tc, qT, k_words, k_scales, vT, vs, offs, out):
         key_scales = [[first_scales[:, 0:HALF], first_scales[:, HALF:SLOTS]], []]
         for o in range(PASSES):
             for b in range(Q_BLOCKS):
-                grouped = sb.tile([P, P, PACK], BF16, name=f"q_grouped{o}{b}", tag=f"q_grouped{o}{b}", align_bytes=64)
+                place = (Q_BLOCKS * o + b) % 3
+                grouped = reused.tile(
+                    [P, P, PACK], BF16, name=f"q_grouped{o}{b}", align_bytes=64, offset=place * ROUNDED_BYTES
+                )
                 rounded = grouped[:].rearrange("p (c i) t -> p c t i", i=4)
                 raw = q_raw[o][:, :, b * P : (b + 1) * P].rearrange("p t (c i) -> p c t i", i=4)
-                bias = zero_bias[:] if (o, b) == (0, 0) else vs_cols[:, 0, 0:1]
-                nc.scalar.activation(rounded, raw, ACT.Identity, bias=bias)
+                nc.scalar.copy(rounded, raw)
                 codes, scales = quantize(nc, sb, grouped, f"q{o}{b}")
                 if o == 0:
                     half = sb.tile(
-                        [P, HALF], U8, name=f"second_scales{b}", tag=("zero_bias", "q_raw0")[b], align_bytes=64
+                        [P, HALF], U8, name=f"second_scales{b}", tag=("vs_cols", "q_raw0")[b], align_bytes=64
                     )
                     half_list = offsets[:, b * HALF // 16 : (b + 1) * HALF // 16]
                     nc.vector.tensor_copy(half[:], scale_pool[:, 1, :].bitcast(U8).indirect(half_list))
@@ -130,8 +132,11 @@ def tile_attend_cap_srt_kernel(tc, qT, k_words, k_scales, vT, vs, offs, out):
                     )
 
         v_slots = []
-        for h, tag in enumerate(("q_raw1", "q_grouped11")):
-            g = sb.tile([P, SLOTS], BF16, name=f"v_slots{h}", tag=tag, align_bytes=64)
+        for h in range(V_BLOCKS):
+            if h == 0:
+                g = sb.tile([P, SLOTS], BF16, name="v_slots0", tag="q_raw1", align_bytes=64)
+            else:
+                g = reused.tile([P, SLOTS], BF16, name="v_slots1", align_bytes=64, offset=0)
             first = SCALAR_SHARE if h == 0 else 0
             if first:
                 nc.scalar.activation(g[:, 0:first], v_pool[h][:].indirect(offsets[:, 0 : first // 16]), ACT.Copy)

@@ -90,11 +90,15 @@ def tile_attend_cap_srt_kernel(tc, qT, k_words, k_scales, vT, vs, offs, out):
             nc.tensor.transpose(vs_spread[:, t * P : (t + 1) * P], vs_cols[:, t, :].to_broadcast([P, P]), ident[:])
 
         key_pairs = sb.tile([P, SLOTS], U32, name="key_pairs")
-        nc.vector.tensor_copy(key_pairs[:], key_pool[:].bitcast(U32).indirect(offsets[:]))
         key_words = sb.tile([P, PASSES, 2 * SLOTS], U8, name="key_words", align_bytes=64)
-        nc.vector.tensor_copy(
-            key_words[:].bitcast(U16), key_pairs[:].bitcast(U16).rearrange("p (n h) -> p h n", h=PASSES)
-        )
+        for a in range(2):
+            half_list = offsets[:, a * HALF // 16 : (a + 1) * HALF // 16]
+            nc.vector.tensor_copy(key_pairs[:, a * HALF : (a + 1) * HALF], key_pool[:].bitcast(U32).indirect(half_list))
+        for a in range(2):
+            nc.vector.tensor_copy(
+                key_words[:, :, 2 * a * HALF : 2 * (a + 1) * HALF].bitcast(U16),
+                key_pairs[:, a * HALF : (a + 1) * HALF].bitcast(U16).rearrange("p (n h) -> p h n", h=PASSES),
+            )
 
         scores = [
             [ps.tile([P, HALF], F32, name=f"scores{b}{a}", tag=f"bank{2 * b + a}") for a in range(2)]

from contextlib import ExitStack

import concourse.mybir as mybir
from concourse.masks import make_identity

NQ, SLOTS, TOKENS, D, DV = 256, 512, 1024, 1024, 256
CAP = 2.0
FLOPS = 2 * NQ * SLOTS * (D + DV)

F32 = mybir.dt.float32
BF16 = mybir.dt.bfloat16
I32 = mybir.dt.int32
U32 = mybir.dt.uint32
U16 = mybir.dt.uint16
U8 = mybir.dt.uint8
FP8X4 = mybir.dt.float8_e4m3fn_x4
FP4X4 = mybir.dt.float4_e2m1fn_x4
ACT = mybir.ActivationFunctionType
ALU = mybir.AluOpType

P = 128
PACK = 4
K_PASS = P * PACK
PASSES = D // K_PASS
Q_BLOCKS = NQ // P
V_BLOCKS = DV // P
HALF = SLOTS // 2
ROUNDED_BYTES = 2 * K_PASS
SCALAR_SHARE = 192


def quantize(nc, sb, grouped, name):
    width = grouped.shape[1]
    codes = sb.tile([P, width], U32, name=name + "_codes", align_bytes=64)
    scales = sb.tile([P, width], U8, name=name + "_scales", align_bytes=64)
    nc.vector.quantize_mx(
        out=codes[:].bitcast(FP8X4), scales=scales[:], in_=grouped[:].rearrange("p c t -> p (c t)")
    )
    return codes, scales


def tile_attend_cap_srt_kernel(tc, qT, k_words, k_scales, vT, vs, offs, out):
    nc = tc.nc
    with ExitStack() as ctx:
        sb = ctx.enter_context(tc.tile_pool(name="sb", bufs=1))
        reused = ctx.enter_context(tc.tile_pool(name="reused", bufs=1))
        ps = ctx.enter_context(tc.psum_pool(name="ps", bufs=1))

        vs_pool = sb.tile([P, TOKENS], F32, name="vs_pool")
        nc.scalar.dma_start(vs_pool[P - 1 : P, :], vs[0:1, :])

        offsets = sb.tile([P, SLOTS // 16], U16, name="offsets")
        nc.sync.dma_start(offsets[:], offs)

        key_pool = sb.tile([P, TOKENS], I32, name="key_pool")
        nc.sync.dma_start(key_pool[:], k_words[0].rearrange("p t b -> p (t b)").bitcast(I32))

        scale_pool = sb.tile([P, PASSES, TOKENS // 4], I32, name="scale_pool")
        nc.vector.memset(scale_pool[:], 0)
        ident = sb.tile([P, P], F32, name="ident")
        nc.vector.memset(ident[:], 0.0)
        make_identity(nc, ident[:], nomemset=True)
        nc.vector.memset(vs_pool[0 : P - 1, :], 0.0)
        for row in range(4):
            nc.sync.dma_start(
                scale_pool[row:P:32, :, :],
                k_scales[:, row::4, :].rearrange("o f t -> f o t").bitcast(I32),
            )

        q_raw = []
        for o in range(PASSES):
            t = sb.tile([P, PACK, NQ], F32, name=f"q_raw{o}", tag=f"q_raw{o}", align_bytes=64)
            nc.sync.dma_start(t[:], qT[0, o * K_PASS : (o + 1) * K_PASS, :].rearrange("(p j) w -> p j w", j=PACK))
            q_raw.append(t)
        v_pool = []
        for h in range(V_BLOCKS):
            t = sb.tile([P, TOKENS], F32, name=f"v_pool{h}", tag=f"v_pool{h}", align_bytes=64)
            nc.sync.dma_start(t[:], vT[h * P : (h + 1) * P, :])
            v_pool.append(t)

        vs_slots = reused.tile([P, SLOTS], F32, name="vs_slots", align_bytes=64, offset=ROUNDED_BYTES - 64)
        nc.vector.tensor_copy(vs_slots[:], vs_pool[:].indirect(offsets[:]))
        vs_turned = ps.tile([P, PACK, P], F32, name="vs_turned", tag="bank4")
        for t in range(PACK):
            nc.tensor.transpose(vs_turned[:, t, :], vs_slots[:, t * P : (t + 1) * P], ident[:])
        vs_cols = sb.tile([P, PACK, 1], F32, name="vs_cols", tag="vs_cols", align_bytes=64)
        nc.scalar.copy(vs_cols[:], vs_turned[:, :, P - 1 : P])
        vs_spread = ps.tile([P, SLOTS], F32, name="vs_spread", tag="bank4")
        for t in range(PACK):
            nc.tensor.transpose(vs_spread[:, t * P : (t + 1) * P], vs_cols[:, t, :].to_broadcast([P, P]), ident[:])

        key_pairs = sb.tile([P, SLOTS], U32, name="key_pairs")
        key_words = sb.tile([P, PASSES, 2 * SLOTS], U8, name="key_words", align_bytes=64)
        for a in range(2):
            half_list = offsets[:, a * HALF // 16 : (a + 1) * HALF // 16]
            nc.vector.tensor_copy(key_pairs[:, a * HALF : (a + 1) * HALF], key_pool[:].bitcast(U32).indirect(half_list))
        for a in range(2):
            nc.vector.tensor_copy(
                key_words[:, :, 2 * a * HALF : 2 * (a + 1) * HALF].bitcast(U16),
                key_pairs[:, a * HALF : (a + 1) * HALF].bitcast(U16).rearrange("p (n h) -> p h n", h=PASSES),
            )

        scores = [
            [ps.tile([P, HALF], F32, name=f"scores{b}{a}", tag=f"bank{2 * b + a}") for a in range(2)]
            for b in range(Q_BLOCKS)
        ]
        first_scales = sb.tile([P, SLOTS], U8, name="first_scales", align_bytes=64)
        nc.vector.tensor_copy(first_scales[:], scale_pool[:, 0, :].bitcast(U8).indirect(offsets[:]))
        key_scales = [[first_scales[:, 0:HALF], first_scales[:, HALF:SLOTS]], []]
        for o in range(PASSES):
            for b in range(Q_BLOCKS):
                place = (Q_BLOCKS * o + b) % 3
                grouped = reused.tile(
                    [P, P, PACK], BF16, name=f"q_grouped{o}{b}", align_bytes=64, offset=place * ROUNDED_BYTES
                )
                rounded = grouped[:].rearrange("p (c i) t -> p c t i", i=4)
                raw = q_raw[o][:, :, b * P : (b + 1) * P].rearrange("p t (c i) -> p c t i", i=4)
                nc.scalar.copy(rounded, raw)
                codes, scales = quantize(nc, sb, grouped, f"q{o}{b}")
                if o == 0:
                    half = sb.tile(
                        [P, HALF], U8, name=f"second_scales{b}", tag=("vs_cols", "q_raw0")[b], align_bytes=64
                    )
                    half_list = offsets[:, b * HALF // 16 : (b + 1) * HALF // 16]
                    nc.vector.tensor_copy(half[:], scale_pool[:, 1, :].bitcast(U8).indirect(half_list))
                    key_scales[1].append(half[:])
                for a in range(2):
                    nc.tensor.matmul_mx(
                        out=scores[b][a][:],
                        lhsT=codes[:].bitcast(FP8X4),
                        lhsT_scale=scales[:],
                        rhs=key_words[:, o, 2 * a * HALF : 2 * (a + 1) * HALF].bitcast(FP4X4),
                        rhs_scale=key_scales[o][a],
                        start=(o == 0),
                        stop=(o == PASSES - 1),
                    )

        v_slots = []
        for h in range(V_BLOCKS):
            if h == 0:
                g = sb.tile([P, SLOTS], BF16, name="v_slots0", tag="q_raw1", align_bytes=64)
            else:
                g = reused.tile([P, SLOTS], BF16, name="v_slots1", align_bytes=64, offset=0)
            first = SCALAR_SHARE if h == 0 else 0
            if first:
                nc.scalar.activation(g[:, 0:first], v_pool[h][:].indirect(offsets[:, 0 : first // 16]), ACT.Copy)
            nc.vector.tensor_copy(g[:, first:SLOTS], v_pool[h][:].indirect(offsets[:, first // 16 : SLOTS // 16]))
            v_slots.append(g)
        v_turned = ps.tile([P, V_BLOCKS, 2, P], F32, name="v_turned", tag="bank5")
        for h in range(V_BLOCKS):
            pairs = v_slots[h][:].bitcast(F32)
            for u in range(2):
                nc.tensor.transpose(v_turned[:, h, u, :], pairs[:, u::2], ident[:])

        capped, neg_max = [], []
        for b in range(Q_BLOCKS):
            c = sb.tile([P, 2, P, 2], F32, name=f"capped{b}", tag=f"capped{b}", align_bytes=64)
            for a in range(2):
                nc.scalar.activation(
                    c[:, :, a * P // 2 : (a + 1) * P // 2, :],
                    scores[b][a][:].rearrange("q (s u e) -> q u s e", u=2, e=2),
                    ACT.Tanh,
                    scale=1.0 / CAP,
                )
            m = sb.tile([P, 1], F32, name=f"neg_max{b}")
            nc.vector.tensor_reduce(
                m[:], c[:].rearrange("q u s e -> q (u s e)"), mybir.AxisListType.X, ALU.max, negate=True
            )
            capped.append(c)
            neg_max.append(m)

        total = sb.tile([P, 2, Q_BLOCKS], F32, name="total")
        shift = sb.tile([P, Q_BLOCKS], F32, name="shift")
        vs_halves = vs_spread[:].rearrange("q (s u e) -> q u s e", u=2, e=2)
        w_turned = []
        for b in range(Q_BLOCKS):
            w = sb.tile([P, 2, P, 2], BF16, name=f"w{b}", align_bytes=64)
            turned = ps.tile([P, 2, P], F32, name=f"w_turned{b}")
            nc.scalar.activation(shift[:, b : b + 1], neg_max[b][:], ACT.Exp, scale=CAP)
            for u in range(2):
                if b == 0:
                    grown = sb.tile([P, P, 2], F32, name=f"grown{u}", tag=f"grown{u}", align_bytes=64)[:]
                else:
                    grown = capped[u][:, 0]
                nc.scalar.activation(grown, capped[b][:, u], ACT.Exp, scale=CAP, accum_out=total[:, u, b : b + 1])
                nc.vector.scalar_tensor_tensor(
                    w[:, u], grown, shift[:, b : b + 1], vs_halves[:, u], op0=ALU.mult, op1=ALU.mult
                )
                nc.tensor.transpose(turned[:, u, :], w[:, u].rearrange("q s e -> q (s e)").bitcast(F32), ident[:])
            w_turned.append(turned)

        inv = sb.tile([P, Q_BLOCKS], F32, name="inv")
        nc.vector.tensor_tensor(total[:, 0, :], total[:, 0, :], total[:, 1, :], ALU.add)
        v_grouped = sb.tile([P, V_BLOCKS, P, 2], F32, name="v_grouped", tag="grown1", align_bytes=64)
        nc.scalar.copy(v_grouped[:], v_turned[:].rearrange("s h u e -> s h e u"))
        w_grouped = []
        for b in range(Q_BLOCKS):
            w_grouped.append(sb.tile([P, P, 2], F32, name=f"w_grouped{b}", tag=f"w_grouped{b}", align_bytes=64))
        nc.vector.tensor_tensor(total[:, 1, :], total[:, 0, :], shift[:], ALU.mult)
        v_codes = sb.tile([P, DV], U32, name="v_codes", align_bytes=64)
        v_scales = sb.tile([P, DV], U8, name="v_scales", align_bytes=64)
        nc.vector.quantize_mx(
            out=v_codes[:].bitcast(FP8X4),
            scales=v_scales[:],
            in_=v_grouped[:].rearrange("s h e u -> s (h e u)").bitcast(BF16),
        )
        nc.vector.reciprocal(inv[:], total[:, 1, :])

        w_quantized = []
        for b in range(Q_BLOCKS):
            codes = sb.tile([P, P], U32, name=f"w_codes{b}", align_bytes=64)
            scales = sb.tile([P, P], U8, name=f"w_scales{b}", align_bytes=64)
            pieces = b + 1
            for piece in range(pieces):
                rows = slice(piece * P // pieces, (piece + 1) * P // pieces)
                grouped = w_grouped[b][:, rows, :]
                nc.scalar.copy(grouped, w_turned[b][:, :, rows].rearrange("s u q -> s q u"))
                nc.vector.quantize_mx(
                    out=codes[:, rows].bitcast(FP8X4),
                    scales=scales[:, rows],
                    in_=grouped.rearrange("s q u -> s (q u)").bitcast(BF16),
                )
            w_quantized.append((codes, scales))

        for b in range(Q_BLOCKS):
            w_codes, w_scales = w_quantized[b]
            res = sb.tile([P, DV], F32, name=f"res{b}", tag=f"w_grouped{1 - b}", align_bytes=64)
            for h in range(V_BLOCKS):
                cols = slice(h * P, (h + 1) * P)
                y = ps.tile([P, P], F32, name=f"y{b}{h}", tag=f"bank{2 * b + h}")
                nc.tensor.matmul_mx(
                    out=y[:],
                    lhsT=w_codes[:].bitcast(FP8X4),
                    lhsT_scale=w_scales[:],
                    rhs=v_codes[:, cols].bitcast(FP8X4),
                    rhs_scale=v_scales[:, cols],
                    start=True,
                    stop=True,
                )
                if h == 1:
                    nc.vector.tensor_scalar(res[:, cols], y[:], inv[:, b : b + 1], None, op0=ALU.mult)
                else:
                    nc.scalar.activation(res[:, cols], y[:], ACT.Copy, scale=inv[:, b : b + 1])
            nc.sync.dma_start(out[0, b * P : (b + 1) * P, :], res[:])
